import numpy as np, ml_dtypes
CORES = [14,30,46,142,158,174,270,286,302,398,414,430]
N = 12
S, T = 8192, 512
def entries(a): return a.T.reshape(-1)
def pack(v, P): return np.ascontiguousarray(np.asarray(v, np.int32).reshape(-1, P).T)
def lists(rng, how):
    M = rng.integers(0, S, (N, S)); b = rng.integers(0, S, T)
    if how == "alike": M = np.stack([rng.permutation(S) for f in range(N)]); b[:] = rng.integers(S)
    if how == "edge":
        M = np.where(rng.random((N, S)) < 0.5, 0, S - 1); w = rng.permutation(N) % 2 * (S - 1); M[:, 0] = w; M[:, S - 1] = S - 1 - w
        b = np.where(rng.random(T) < 0.5, 0, S - 1); b[rng.permutation(T)[:2]] = [0, S - 1]
    if how == "fold":
        V = np.stack([rng.permutation(S)[:4] for f in range(N + 1)]); M = V[np.arange(N)[:, None], rng.integers(0, 4, (N, S))]
        M[np.arange(N)[:, None], V[1:]] = V[:N]; b[rng.permutation(T)[:4]] = V[N]
    if how == "mixed":
        k = np.concatenate([[3, 3], rng.permutation(np.arange(N - 2) % 3)])
        for f in range(N): M[f] = [np.arange(S), rng.permutation(S), M[f], rng.integers(0, S, 4)[rng.integers(0, 4, S)]][k[f]]
    if how == "turn": M = np.stack([rng.permutation(S) for f in range(N)]); b = rng.permutation(S)[:T]
    return {"bp": np.stack([pack(m, 16) for m in M]), "st": np.broadcast_to(pack(b, 16), (N, 16, T // 16)).copy()}
def setup_inputs(rng):
    return dict({"tab": rng.standard_normal((N, 128, S), dtype=np.float32).astype(ml_dtypes.bfloat16)}, **lists(rng, "uniform"))
def setup_inputs_alike(rng):
    d = setup_inputs(rng); d.update(lists(rng, "alike"))
    for k in ("tab",): d[k] = (d[k].astype(np.float32) * 1048576.0).astype(d[k].dtype)
    return d
def setup_inputs_edge(rng):
    d = setup_inputs(rng); d.update(lists(rng, "edge"))
    for k in ("tab",): d[k] = (d[k].astype(np.float32) * (1 / 1024.0)).astype(d[k].dtype)
    return d
def setup_inputs_fold(rng):
    d = setup_inputs(rng); d.update(lists(rng, "fold"))
    return d
def setup_inputs_mixed(rng):
    d = setup_inputs(rng); d.update(lists(rng, "mixed"))
    return d
def setup_inputs_turn(rng):
    d = setup_inputs(rng); d.update(lists(rng, "turn"))
    return d
def check_inputs(x):
    bad = []
    if x["bp"].min() < 0 or x["bp"].max() >= S: bad.append("bp out of range")
    if x["st"].min() < 0 or x["st"].max() >= S: bad.append("st out of range")
    if not all(np.array_equal(a, x["st"][0]) for a in x["st"]): bad.append("st isn't alike on all ranks")
    return bad
def reference(tab, bp, st):
    b = entries(st[0]); y = np.zeros((N, 128, T), tab.dtype)
    for f in range(N - 1, -1, -1):
        y[f] = tab[f][:, b]
        b = entries(bp[f])[b]
    return {"y": y}

@@ -1,0 +1,398 @@
+from concourse.bass import DstId, RemoteDMATransfer
+from concourse.mybir import AluOpType, ActivationFunctionType
+
+EQ, MUL, ADD = AluOpType.is_equal, AluOpType.mult, AluOpType.add
+SHR, AND = AluOpType.arith_shift_right, AluOpType.bitwise_and
+
+SCRATCH = {
+    "tabs": ("sbuf", [128, 8192], "bfloat16"),
+    "win": ("sbuf", [128, 8192], "bfloat16"),
+    "bps": ("sbuf", [128, 64], "int32"),
+    "spa": ("sbuf", [128, 64], "int32"),
+    "spb": ("sbuf", [128, 64], "int32"),
+    "pca": ("sbuf", [128, 64], "bfloat16"),
+    "pcb": ("sbuf", [128, 64], "bfloat16"),
+    "mine": ("dram", [128, 128], "bfloat16"),
+    "land": ("dram", [640, 128], "bfloat16"),
+    "lsta": ("sbuf", [128, 8], "uint16"),
+    "lstb": ("sbuf", [128, 4], "uint16"),
+    "ofl": ("sbuf", [128, 32], "uint16"),
+    "ysb": ("sbuf", [128, 512], "bfloat16"),
+    "gat": ("sbuf", [128, 640], "bfloat16"),
+    "rw": ("sbuf", [128, 200], "bfloat16"),
+    "off_a": ("sbuf", [128, 40], "uint16"),
+    "off_b": ("sbuf", [128, 20], "uint16"),
+    "ps": ("psum", [128, 2560], "float32"),
+    "xf": ("sbuf", [128, 64], "float32"),
+    "of": ("sbuf", [128, 64], "uint16"),
+    "pf": ("psum", [128, 1024], "float32"),
+    "kcol": ("sbuf", [128, 1], "int32"),
+    "kpar": ("sbuf", [128, 1], "int32"),
+    "wlist": ("sbuf", [128, 1], "float32"),
+    "wnat": ("sbuf", [128, 1], "float32"),
+    "ia": ("sbuf", [128, 36], "int32"),
+    "ja": ("sbuf", [128, 36], "int32"),
+    "ib": ("sbuf", [128, 40], "int32"),
+    "jb": ("sbuf", [128, 40], "int32"),
+    "iba": ("sbuf", [128, 32], "int32"),
+    "jba": ("sbuf", [128, 32], "int32"),
+    "bma": ("sbuf", [128, 32], "float32"),
+    "ibb": ("sbuf", [128, 32], "int32"),
+    "jbb": ("sbuf", [128, 32], "int32"),
+    "bmb": ("sbuf", [128, 32], "float32"),
+    "ipm": ("sbuf", [128, 128], "int32"),
+    "jpm": ("sbuf", [128, 128], "int32"),
+    "pm": ("sbuf", [128, 128], "float32"),
+    "bpw": ("sbuf", [128, 512], "int32"),
+    "w0": ("sbuf", [128, 4], "int32"),
+    "w0h": ("sbuf", [128, 4], "int32"),
+    "w0l": ("sbuf", [128, 4], "int32"),
+    "off0": ("sbuf", [128, 4], "uint16"),
+    "low": ("sbuf", [128, 4], "float32"),
+    "qi": ("sbuf", [128, 1], "int32"),
+    "qcol": ("sbuf", [128, 1], "float32"),
+    "e16": ("sbuf", [128, 16], "bfloat16"),
+    "iblk": ("sbuf", [128, 128], "int32"),
+    "jblk": ("sbuf", [128, 128], "int32"),
+    "blk": ("sbuf", [128, 128], "bfloat16"),
+    "ir": ("sbuf", [128, 48], "int32"),
+    "jr": ("sbuf", [128, 48], "int32"),
+    "r11": ("sbuf", [128, 48], "float32"),
+    "xl": ("sbuf", [128, 64], "bfloat16"),
+    "mask": ("sbuf", [128, 64], "float32"),
+    "m11": ("sbuf", [128, 64], "float32"),
+    "bq": ("sbuf", [128, 8], "int32"),
+    "tq": ("sbuf", [128, 8], "float32"),
+    "oq": ("sbuf", [128, 8], "float32"),
+    "st16": ("sbuf", [16, 32], "int32"),
+    "stf": ("sbuf", [16, 32], "float32"),
+}
+
+SEMAPHORES = ["e%d" % _i for _i in range(90)] + ["arr%d" % _i for _i in range(5)] + ["larr", "oarr", "sentm", "sentl"]
+
+WALK = {9: [10, 9, 8, 7, 6], 8: [10, 9], 7: [10, 9, 8], 6: [10, 9, 8, 7, 6],
+        4: [5], 3: [5, 4], 2: [5, 4, 3], 1: [5, 4, 3, 2], 0: [5, 4, 3, 2, 1]}
+SLOT = {9: 0, 7: 1, 10: 2, 8: 3, 6: 4, 5: 0, 3: 1, 1: 2, 4: 3, 2: 4}
+MAPS_TO = {10: [[9], [6, 8, 7]], 9: [[6], [8, 7]], 8: [[9], [6, 7]], 7: [[9], [6]], 6: [[9]],
+           5: [[0], [1, 2, 3, 4]], 4: [[0], [1, 2, 3]], 3: [[0], [1, 2]], 2: [[0], [1]], 1: [[0]]}
+LIST_TO = {11: [[9], [6, 7, 8]], 9: [[0], [1, 2]], 6: [[3, 4]]}
+OFFS_TO = {11: 10, 6: 5}
+TAB_EARLY = {9: 4, 6: 2, 10: 1, 8: 1, 7: 1, 11: 0, 0: 4}
+TAB_MID = {5: 6, 4: 2, 3: 2, 2: 2, 1: 2, 10: 7}
+
+
+def rank_program(g, core, T, topo):
+    me = T.rank_of(core)
+    if me is None:
+        return
+    V, S, PE, Y = g.vector, g.scalar, g.tensor, g.sync
+    events = []
+
+    def ev():
+        e = {"s": T.sem["e%d" % len(events)], "n": 0, "w": 0}
+        events.append(e)
+        return e
+
+    def inc(op, e, n=1):
+        op.then_inc(e["s"], n)
+        e["n"] += n
+
+    def wait(q, *es):
+        for e in es:
+            if e["n"]:
+                q.wait_ge(e["s"], e["n"])
+                e["w"] = e["n"]
+
+    sent = {"sentm": 0, "sentl": 0}
+
+    def send(dsts, out, in_, rsem, lsem):
+        cores = [T.cores[d] for d in dsts]
+        m = topo.mask(core, cores[0])
+        for c in cores:
+            m &= topo.mask(core, c)
+        ids = []
+        for c in cores:
+            rid, pid = topo.addr(c, core)
+            ids.append(DstId(rid=rid, pnc=pid))
+        g.remote_dma_fused([RemoteDMATransfer(dst_ids=ids, dma_engine_mask=m, remote_sem=T.sem[rsem],
+                                              srcs=[in_], dsts=[out] * len(ids))], local_sem=T.sem[lsem])
+        sent[lsem] += bin(m).count("1")
+
+    def arrived(src):
+        return bin(topo.mask(T.cores[src], core)).count("1")
+
+    walk = WALK.get(me, [])
+    has_map = 1 <= me <= 10
+    own = me in walk
+    first = walk[:1] == [10]
+
+    e_tab = ev()
+    tab_at = [0]
+
+    def tab_load(units):
+        a = tab_at[0]
+        b = min(8192, a + 1024 * units)
+        if b > a:
+            inc(Y.dma_start(T.tabs[:, a:b], T.tab[:, a:b]), e_tab, 16)
+        tab_at[0] = b
+
+    e_bp, e_st, e_bpw, e_st16 = ev(), ev(), ev(), ev()
+    if has_map:
+        inc(Y.dma_start(T.bps[:], T.bp[:]), e_bp, 16)
+    if me == 11:
+        for q, gs in ((Y, (0, 1, 2, 3)), (S, (4, 5, 6, 7))):
+            for k in gs:
+                inc(q.dma_start(T.w0[16 * k:16 * k + 16, :], T.st[:, 4 * k:4 * k + 4]), e_st, 16)
+            for k in gs:
+                inc(q.dma_start(T.bpw[16 * k:16 * k + 16, :], T.bp[:]), e_bpw, 16)
+        inc(Y.dma_start(T.st16[:], T.st[:]), e_st16, 16)
+    tab_load(TAB_EARLY.get(me, 2))
+
+    e_io = ev()
+    fin = []
+    if walk:
+        fin = [len(walk) - 1, walk.index(7)] if me == 6 else [walk.index(me + 1)]
+    forms = set("b" if walk[t] % 2 == 0 else "a" for t in fin)
+    if me == 11:
+        forms = {"a"}
+    if walk or me == 11:
+        inc(g.iota(T.kcol[:], [[0, 1]], 0, 1), e_io)
+        inc(g.iota(T.ipm[:], [[1, 128]], 128, -1), e_io)
+        if "a" in forms:
+            inc(g.iota(T.iba[:], [[0, 8], [16, 4]], 15, -1), e_io)
+        if "b" in forms:
+            inc(g.iota(T.ibb[:], [[16, 8], [0, 4]], 15, -1), e_io)
+    if walk:
+        inc(g.iota(T.ia[:], [[0, 9], [16, 4]], 1, -1), e_io)
+        inc(g.iota(T.ib[:, 0:8], [[16, 8]], 1, -1), e_io)
+        inc(g.iota(T.ib[:, 8:40], [[16, 8], [0, 4]], 1, -1), e_io)
+    if me == 11:
+        inc(g.iota(T.iblk[:], [[16, 8], [0, 16]], 15, -1), e_io)
+        inc(g.iota(T.ir[:, 0:16], [[0, 2], [16, 8]], 15, -1), e_io)
+        inc(g.iota(T.ir[:, 16:48], [[16, 8], [0, 4]], 15, -1), e_io)
+
+    e_win = ev()
+    e_sa, e_sb, e_pa, e_pb, e_store = ev(), ev(), ev(), ev(), ev()
+    if walk:
+        inc(V.memset(T.win[:, 0:4096], 0.0), e_win)
+    if has_map:
+        wait(V, e_bp)
+        inc(V.tensor_scalar(T.spa[:], T.bps[:], 15, None, AND), e_sa)
+        inc(V.tensor_scalar(T.spb[:], T.bps[:], 4, None, SHR), e_sb)
+        wait(V, e_sa)
+        inc(V.tensor_copy(T.pca[:], T.spa[:]), e_pa)
+        wait(V, e_sb)
+        inc(V.tensor_scalar(T.pcb[:], T.spb[:], -256.0, None, ADD), e_pb)
+        wait(Y, e_pa)
+        inc(Y.dma_start(T.mine[0:64, :], T.pca[:]), e_store, 16)
+        wait(S, e_pb)
+        inc(S.dma_start(T.mine[64:128, :], T.pcb[:]), e_store, 16)
+        wait(g, e_store)
+        r = SLOT[me]
+        for dsts in MAPS_TO[me]:
+            send(dsts, T.land[128 * r:128 * r + 128, :], T.mine[:], "arr%d" % r, "sentm")
+    if walk:
+        inc(V.memset(T.win[:, 4096:8192], 0.0), e_win)
+
+    e_c1, e_c2, e_c3 = ev(), ev(), ev()
+    rows = {"a": 64, "b": 128}
+    if walk or me == 11:
+        wait(V, e_io)
+        inc(V.tensor_scalar(T.jpm[:], T.ipm[:], 15, None, AND), e_c1)
+        for f in sorted(forms):
+            inc(V.tensor_scalar(T["jb" + f][:], T["ib" + f][:], 4, None, SHR), e_c1)
+        if walk:
+            inc(V.tensor_scalar(T.kpar[:], T.kcol[:], 1, None, AND), e_c1)
+            inc(V.tensor_scalar(T.ja[:], T.ia[:], 1, None, SHR), e_c1)
+            inc(V.tensor_scalar(T.jb[:], T.ib[:], 1, None, SHR), e_c1)
+        else:
+            inc(V.tensor_scalar(T.qi[:], T.kcol[:], 15, None, AND), e_c1)
+            inc(V.tensor_scalar(T.jblk[:], T.iblk[:], 4, None, SHR), e_c1)
+            inc(V.tensor_scalar(T.jr[:], T.ir[:], 4, None, SHR), e_c1)
+        wait(V, e_c1)
+        if walk:
+            inc(V.tensor_scalar(T.wlist[:], T.kpar[:], -511.0, 512.0, MUL, ADD), e_c2)
+            inc(V.tensor_scalar(T.wnat[:], T.kpar[:], 15.0, 1.0, MUL, ADD), e_c2)
+        else:
+            inc(V.tensor_copy(T.qcol[:], T.qi[:]), e_c2)
+            inc(V.tensor_scalar(T.blk[:], T.jblk[:], 0.0, None, EQ), e_c2)
+            inc(V.tensor_scalar(T.e16[:], T.jpm[:, 0:16], 0.0, None, EQ), e_c2)
+            inc(V.tensor_scalar(T.r11[:, 0:8], T.jr[:, 0:8], 0.0, None, EQ), e_c2)
+            inc(V.tensor_scalar(T.r11[:, 8:16], T.jr[:, 8:16], 0.0, 512.0, EQ, MUL), e_c2)
+            inc(V.tensor_scalar(T.r11[:, 16:48], T.jr[:, 16:48], 0.0, None, EQ), e_c2)
+        inc(V.tensor_scalar(T.pm[:], T.jpm[:], 0.0, None, EQ), e_c3)
+        for f in sorted(forms):
+            inc(V.tensor_scalar(T["bm" + f][:], T["jb" + f][:], 0.0, None, EQ), e_c3)
+        wait(V, e_c2)
+    if walk:
+        for t, m in enumerate(walk):
+            j, w, n = (T.ja, 4, 36) if m % 2 == 0 else (T.jb, 8, 40)
+            r = SLOT[m]
+            inc(V.tensor_scalar(T.rw[:, 40 * t:40 * t + w], j[:, 0:w], float(-r), T.wlist[:, 0:1], EQ, MUL), e_c3)
+            if t in fin:
+                inc(V.tensor_scalar(T.rw[:, 40 * t + w:40 * t + n], j[:, w:n], float(-r), T.wnat[:, 0:1], EQ, MUL), e_c3)
+            if m % 2:
+                inc(V.memset(T.off_a[64:128, 8 * t:8 * t + 8], 0), e_c3)
+
+    e_wdma = ev()
+    if has_map and TAB_MID.get(me):
+        Y.wait_ge(T.sem.sentm, sent["sentm"])
+        tab_load(TAB_MID[me])
+
+    def fill(q, gp, r0, r1, src):
+        inc(q.dma_start(T.win[16 * gp + 2 * r0:16 * gp + 2 * r1, :], src), e_wdma, 16)
+
+    def groups_of(m):
+        return range(8) if m % 2 else range(4)
+
+    if walk:
+        wait(Y, e_win)
+        wait(S, e_win)
+        if own:
+            wait(Y, e_store)
+            wait(S, e_store)
+            for gp in groups_of(me):
+                fill((Y, S)[gp % 2], gp, SLOT[me], SLOT[me] + 1, T.mine[:])
+        got = [m for m in walk if m != me]
+        for m in got:
+            for q in (Y, S):
+                q.wait_ge(T.sem["arr%d" % SLOT[m]], arrived(m))
+        for gp in range(8):
+            rs = sorted(SLOT[m] for m in got if gp in groups_of(m))
+            i = 0
+            while i < len(rs):
+                k = i
+                while k + 1 < len(rs) and rs[k + 1] == rs[k] + 1:
+                    k += 1
+                fill((Y, S)[gp % 2], gp, rs[i], rs[k] + 1, T.land[128 * rs[i]:128 * (rs[k] + 1), :])
+                i = k + 1
+    if me not in LIST_TO:
+        tab_load(8)
+
+    def finalize(i, t, w, f, addend):
+        k = rows[f]
+        x, pf = T.xf[0:k, 32 * i:32 * i + 32], T.pf[:, 512 * i:512 * i + 32]
+        e1, e2, e3 = ev(), ev(), ev()
+        wait(V, e_c3)
+        inc(V.tensor_tensor(x, T.ps[0:k, 512 * t + w:512 * t + w + 32], T["bm" + f][0:k, :], MUL), e1)
+        wait(PE, e_c3, e1)
+        inc(PE.matmul(pf, T.pm[0:k, :], x, True, True), e2)
+        wait(V, e2)
+        inc(V.tensor_scalar(T.of[:, 32 * i:32 * i + 32], pf, addend, None, ADD), e3)
+        return (T.of, 32 * i), e3
+
+    offs = None
+    e_offs = None
+    if walk:
+        up = 11 if first else (9 if me <= 2 else 6)
+        off, c0 = (T.lsta if first else T.lstb), 0
+        e_off = None
+        wait(PE, e_c3)
+        wait(V, e_c3, e_wdma)
+        wait(S, e_c3, e_wdma)
+        for t, m in enumerate(walk):
+            x = 128 * t
+            even = m % 2 == 0
+            w, k, n = (4, 128, 36) if even else (8, 64, 40)
+            if t not in fin:
+                n = w
+            e_g, e_s, e_m = ev(), ev(), ev()
+            for q in ((V, S) if even else (V,)):
+                if e_off is None:
+                    q.wait_ge(T.sem.larr, arrived(up))
+                else:
+                    wait(q, e_off)
+            inc(V.tensor_copy(T.gat[:, x:x + 64], T.win[:, :].indirect(off[:, c0:c0 + 4])), e_g)
+            if even:
+                inc(S.activation(T.gat[:, x + 64:x + 128], T.win[:, :].indirect(off[:, c0 + 4:c0 + 8]),
+                                 ActivationFunctionType.Copy), e_s)
+            wait(PE, e_g, e_s)
+            inc(PE.matmul(T.ps[0:k, 512 * t:512 * t + n], T.gat[:, x:x + k], T.rw[:, 40 * t:40 * t + n], True, True), e_m)
+            wait(V, e_m)
+            if t < len(walk) - 1 or me in LIST_TO:
+                off, c0 = (T.off_b, 4 * t) if even else (T.off_a, 8 * t)
+                e_off = ev()
+                inc(V.tensor_scalar(off[0:k, c0:c0 + w], T.ps[0:k, 512 * t:512 * t + w], 256.0, None, ADD), e_off)
+        if me in LIST_TO:
+            wait(g, e_off)
+            for dsts in LIST_TO[me]:
+                send(dsts, T.lstb[:], off[:, c0:c0 + 4], "larr", "sentl")
+        for i, t in enumerate(fin):
+            even = walk[t] % 2 == 0
+            o, e = finalize(i, t, 4 if even else 8, "b" if even else "a", 4096.0)
+            if me == 6 and i == 0:
+                wait(g, e)
+                send([OFFS_TO[me]], T.ofl[:], o[0][:, o[1]:o[1] + 32], "oarr", "sentl")
+            else:
+                offs, e_offs = o, e
+
+    if me == 11:
+        e1, e2, e3, e4, e5, e6, e7 = ev(), ev(), ev(), ev(), ev(), ev(), ev()
+        wait(V, e_st)
+        inc(V.tensor_scalar(T.w0l[:], T.w0[:], 15, None, AND), e1)
+        inc(V.tensor_scalar(T.w0h[:], T.w0[:], 4, None, SHR), e2)
+        wait(V, e1)
+        inc(V.tensor_copy(T.low[:], T.w0l[:]), e3)
+        wait(V, e2)
+        inc(V.tensor_copy(T.off0[:], T.w0h[:]), e4)
+        wait(V, e3)
+        for c in range(4):
+            inc(V.tensor_scalar(T.xl[:, 16 * c:16 * c + 16], T.e16[:], T.low[:, c:c + 1], None, MUL), e5)
+        wait(PE, e_c2, e5)
+        inc(PE.matmul(T.ps[:, 512:576], T.blk[:], T.xl[:], True, True), e6)
+        wait(V, e6)
+        inc(V.tensor_scalar(T.mask[:], T.ps[:, 512:576], T.qcol[:, 0:1], None, EQ), e7)
+        h0, h1, h2, h3, h4, h5, h6 = ev(), ev(), ev(), ev(), ev(), ev(), ev()
+        inc(V.memset(T.off_a[64:128, 0:8], 0), h0)
+        wait(V, e7, e4, e_bpw)
+        inc(V.tensor_tensor(T.m11[:], T.bpw[:, :].indirect(T.off0[:, 0:4]), T.mask[:], MUL), h1)
+        wait(PE, h1)
+        inc(PE.matmul(T.ps[0:64, 0:48], T.m11[:], T.r11[:], True, True), h2)
+        wait(V, h2)
+        inc(V.tensor_scalar(T.bq[0:64, :], T.ps[0:64, 0:8], 0.0625, -0.46875, MUL, ADD), h3)
+        wait(V, h3)
+        inc(V.tensor_scalar(T.tq[0:64, :], T.bq[0:64, :], -8191.0, None, MUL), h4)
+        wait(V, h4)
+        inc(V.tensor_tensor(T.oq[0:64, :], T.tq[0:64, :], T.ps[0:64, 8:16], ADD), h5)
+        wait(V, h5)
+        inc(V.tensor_copy(T.off_a[0:64, 0:8], T.oq[0:64, :]), h6)
+        wait(g, h0, h6)
+        for dsts in LIST_TO[me]:
+            send(dsts, T.lsta[:], T.off_a[:, 0:8], "larr", "sentl")
+        o, e = finalize(0, 0, 16, "a", 0.0)
+        wait(g, e)
+        send([OFFS_TO[me]], T.ofl[:], o[0][:, o[1]:o[1] + 32], "oarr", "sentl")
+        k1, k2, k3 = ev(), ev(), ev()
+        wait(V, e_st16)
+        inc(V.tensor_copy(T.stf[:], T.st16[:]), k1)
+        wait(PE, k1)
+        inc(PE.matmul(T.pf[:, 512:544], T.pm[0:16, :], T.stf[:], True, True), k2)
+        wait(V, k2)
+        inc(V.tensor_copy(T.of[:, 32:64], T.pf[:, 512:544]), k3)
+        offs, e_offs = (T.of, 32), k3
+
+    if me in LIST_TO:
+        Y.wait_ge(T.sem.sentl, sent["sentl"])
+        tab_load(8)
+    e_y0, e_y1, e_out = ev(), ev(), ev()
+    for q in (V, S):
+        if offs is None:
+            q.wait_ge(T.sem.oarr, arrived(11 if me == 10 else 6))
+        else:
+            wait(q, e_offs)
+        wait(q, e_tab)
+    o, c0 = (T.ofl, 0) if offs is None else offs
+    inc(V.tensor_copy(T.ysb[:, 0:256], T.tabs[:, :].indirect(o[:, c0:c0 + 16])), e_y0)
+    inc(S.activation(T.ysb[:, 256:512], T.tabs[:, :].indirect(o[:, c0 + 16:c0 + 32]),
+                     ActivationFunctionType.Identity, bias=-0.0), e_y1)
+    wait(Y, e_y0)
+    inc(Y.dma_start(T.y[:, 0:256], T.ysb[:, 0:256]), e_out, 16)
+    wait(S, e_y1)
+    inc(S.dma_start(T.y[:, 256:512], T.ysb[:, 256:512]), e_out, 16)
+    wait(g, e_out)
+    for k in ("sentm", "sentl"):
+        if sent[k]:
+            g.wait_ge(T.sem[k], sent[k])
+    for e in events:
+        if e["w"] < e["n"]:
+            wait(g, e)

@@ -3,82 +3,35 @@ from concourse.mybir import AluOpType, ActivationFunctionType
 
 EQ, MUL, ADD = AluOpType.is_equal, AluOpType.mult, AluOpType.add
 SHR, AND = AluOpType.arith_shift_right, AluOpType.bitwise_and
+COPY = ActivationFunctionType.Copy
 
-SCRATCH = {
-    "tabs": ("sbuf", [128, 8192], "bfloat16"),
-    "win": ("sbuf", [128, 8192], "bfloat16"),
-    "bps": ("sbuf", [128, 64], "int32"),
-    "spa": ("sbuf", [128, 64], "int32"),
-    "spb": ("sbuf", [128, 64], "int32"),
-    "pca": ("sbuf", [128, 64], "bfloat16"),
-    "pcb": ("sbuf", [128, 64], "bfloat16"),
-    "mine": ("dram", [128, 128], "bfloat16"),
-    "land": ("dram", [640, 128], "bfloat16"),
-    "lsta": ("sbuf", [128, 8], "uint16"),
-    "lstb": ("sbuf", [128, 4], "uint16"),
-    "ofl": ("sbuf", [128, 32], "uint16"),
-    "ysb": ("sbuf", [128, 512], "bfloat16"),
-    "gat": ("sbuf", [128, 640], "bfloat16"),
-    "rw": ("sbuf", [128, 200], "bfloat16"),
-    "off_a": ("sbuf", [128, 40], "uint16"),
-    "off_b": ("sbuf", [128, 20], "uint16"),
-    "ps": ("psum", [128, 2560], "float32"),
-    "xf": ("sbuf", [128, 64], "float32"),
-    "of": ("sbuf", [128, 64], "uint16"),
-    "pf": ("psum", [128, 1024], "float32"),
-    "kcol": ("sbuf", [128, 1], "int32"),
-    "kpar": ("sbuf", [128, 1], "int32"),
-    "wlist": ("sbuf", [128, 1], "float32"),
-    "wnat": ("sbuf", [128, 1], "float32"),
-    "ia": ("sbuf", [128, 36], "int32"),
-    "ja": ("sbuf", [128, 36], "int32"),
-    "ib": ("sbuf", [128, 40], "int32"),
-    "jb": ("sbuf", [128, 40], "int32"),
-    "iba": ("sbuf", [128, 32], "int32"),
-    "jba": ("sbuf", [128, 32], "int32"),
-    "bma": ("sbuf", [128, 32], "float32"),
-    "ibb": ("sbuf", [128, 32], "int32"),
-    "jbb": ("sbuf", [128, 32], "int32"),
-    "bmb": ("sbuf", [128, 32], "float32"),
-    "ipm": ("sbuf", [128, 128], "int32"),
-    "jpm": ("sbuf", [128, 128], "int32"),
-    "pm": ("sbuf", [128, 128], "float32"),
-    "bpw": ("sbuf", [128, 512], "int32"),
-    "w0": ("sbuf", [128, 4], "int32"),
-    "w0h": ("sbuf", [128, 4], "int32"),
-    "w0l": ("sbuf", [128, 4], "int32"),
-    "off0": ("sbuf", [128, 4], "uint16"),
-    "low": ("sbuf", [128, 4], "float32"),
-    "qi": ("sbuf", [128, 1], "int32"),
-    "qcol": ("sbuf", [128, 1], "float32"),
-    "e16": ("sbuf", [128, 16], "bfloat16"),
-    "iblk": ("sbuf", [128, 128], "int32"),
-    "jblk": ("sbuf", [128, 128], "int32"),
-    "blk": ("sbuf", [128, 128], "bfloat16"),
-    "ir": ("sbuf", [128, 48], "int32"),
-    "jr": ("sbuf", [128, 48], "int32"),
-    "r11": ("sbuf", [128, 48], "float32"),
-    "xl": ("sbuf", [128, 64], "bfloat16"),
-    "mask": ("sbuf", [128, 64], "float32"),
-    "m11": ("sbuf", [128, 64], "float32"),
-    "bq": ("sbuf", [128, 8], "int32"),
-    "tq": ("sbuf", [128, 8], "float32"),
-    "oq": ("sbuf", [128, 8], "float32"),
-    "st16": ("sbuf", [16, 32], "int32"),
-    "stf": ("sbuf", [16, 32], "float32"),
-}
 
-SEMAPHORES = ["e%d" % _i for _i in range(90)] + ["arr%d" % _i for _i in range(5)] + ["larr", "oarr", "sentm", "sentl"]
+def _sb(dt, **cols):
+    return {k: ("sbuf", [128, n], dt) for k, n in cols.items()}
+
+
+SCRATCH = {"mine": ("dram", [128, 128], "bfloat16"), "land": ("dram", [640, 128], "bfloat16"),
+           "ps": ("psum", [128, 2560], "float32"), "pf": ("psum", [128, 1024], "float32"),
+           "st16": ("sbuf", [16, 32], "int32"), "stf": ("sbuf", [16, 32], "float32")}
+SCRATCH.update(_sb("bfloat16", tabs=8192, win=8192, win2=8192, pc=128, ysb=512, gat=640, rw=400, e16=16, blk=128, xl=64, pmb=128,
+                   pmh=128, xb=128, bma=64, bmb=64))
+SCRATCH.update(_sb("uint16", lsta=8, lstb=4, ofl=32, off_a=40, off_b=20, of=64, off0=4))
+SCRATCH.update(_sb("int32", bps=128, sp=128, kcol=1, kpar=1, ia=68, ja=68, ib=72, jb=72, iba=64, jba=64, ibb=64, jbb=64,
+                   ipm=128, jpm=128, bpw=512, w0=4, w0h=4, w0l=4, qi=1, iblk=128, jblk=128, ir=48, jr=48, bq=8))
+SCRATCH.update(_sb("float32", xf=32, wt=3, bias=1, pm=128, low=4, qcol=1, r11=48, mask=64, m11=64, tq=8, oq=8))
+
+SEMAPHORES = ["e%d" % _i for _i in range(100)] + ["arr%d" % _i for _i in range(5)] + ["larr", "oarr", "sentm", "sentl"]
 
 WALK = {9: [10, 9, 8, 7, 6], 8: [10, 9], 7: [10, 9, 8], 6: [10, 9, 8, 7, 6],
         4: [5], 3: [5, 4], 2: [5, 4, 3], 1: [5, 4, 3, 2], 0: [5, 4, 3, 2, 1]}
-SLOT = {9: 0, 7: 1, 10: 2, 8: 3, 6: 4, 5: 0, 3: 1, 1: 2, 4: 3, 2: 4}
+SLOT = {9: 0, 10: 1, 7: 2, 8: 3, 6: 4, 5: 0, 3: 1, 1: 2, 4: 3, 2: 4}
+TWO = (9, 6)
 MAPS_TO = {10: [[9], [6, 8, 7]], 9: [[6], [8, 7]], 8: [[9], [6, 7]], 7: [[9], [6]], 6: [[9]],
            5: [[0], [1, 2, 3, 4]], 4: [[0], [1, 2, 3]], 3: [[0], [1, 2]], 2: [[0], [1]], 1: [[0]]}
 LIST_TO = {11: [[9], [6, 7, 8]], 9: [[0], [1, 2]], 6: [[3, 4]]}
 OFFS_TO = {11: 10, 6: 5}
-TAB_EARLY = {9: 4, 6: 2, 10: 1, 8: 1, 7: 1, 11: 0, 0: 4}
-TAB_MID = {5: 6, 4: 2, 3: 2, 2: 2, 1: 2, 10: 7}
+TAB_EARLY = {11: 3, 10: 2, 9: 3, 8: 2, 7: 2, 6: 3, 0: 6}
+TAB_MID = {10: 6, 6: 2, 5: 4}
 
 
 def rank_program(g, core, T, topo):
@@ -125,20 +78,23 @@ def rank_program(g, core, T, topo):
     has_map = 1 <= me <= 10
     own = me in walk
     first = walk[:1] == [10]
+    two = me in TWO
 
-    e_tab = ev()
+    e_tab = []
     tab_at = [0]
 
     def tab_load(units):
         a = tab_at[0]
         b = min(8192, a + 1024 * units)
         if b > a:
-            inc(Y.dma_start(T.tabs[:, a:b], T.tab[:, a:b]), e_tab, 16)
+            e_tab.append(ev())
+            inc(Y.dma_start(T.tabs[:, a:b], T.tab[:, a:b]), e_tab[-1], 16)
         tab_at[0] = b
 
     e_bp, e_st, e_bpw, e_st16 = ev(), ev(), ev(), ev()
     if has_map:
-        inc(Y.dma_start(T.bps[:], T.bp[:]), e_bp, 16)
+        inc(Y.dma_start(T.bps[0:64, :], T.bp[:]), e_bp, 16)
+        inc(S.dma_start(T.bps[64:128, :], T.bp[:]), e_bp, 16)
     if me == 11:
         for q, gs in ((Y, (0, 1, 2, 3)), (S, (4, 5, 6, 7))):
             for k in gs:
@@ -146,116 +102,112 @@ def rank_program(g, core, T, topo):
             for k in gs:
                 inc(q.dma_start(T.bpw[16 * k:16 * k + 16, :], T.bp[:]), e_bpw, 16)
         inc(Y.dma_start(T.st16[:], T.st[:]), e_st16, 16)
-    tab_load(TAB_EARLY.get(me, 2))
+    tab_load(TAB_EARLY.get(me, 4))
 
-    e_io = ev()
     fin = []
     if walk:
         fin = [len(walk) - 1, walk.index(7)] if me == 6 else [walk.index(me + 1)]
-    forms = set("b" if walk[t] % 2 == 0 else "a" for t in fin)
-    if me == 11:
-        forms = {"a"}
-    if walk or me == 11:
-        inc(g.iota(T.kcol[:], [[0, 1]], 0, 1), e_io)
-        inc(g.iota(T.ipm[:], [[1, 128]], 128, -1), e_io)
-        if "a" in forms:
-            inc(g.iota(T.iba[:], [[0, 8], [16, 4]], 15, -1), e_io)
-        if "b" in forms:
-            inc(g.iota(T.ibb[:], [[16, 8], [0, 4]], 15, -1), e_io)
+    forms = sorted(set("b" if walk[t] % 2 == 0 else "a" for t in fin))
+    e_k, e_io = ev(), ev()
+    if me != 11:
+        inc(g.iota(T.kcol[:], [[0, 1]], 0, 1), e_k)
     if walk:
-        inc(g.iota(T.ia[:], [[0, 9], [16, 4]], 1, -1), e_io)
+        inc(g.iota(T.ia[:], [[0, 17], [16, 4]], 1, -1), e_io)
         inc(g.iota(T.ib[:, 0:8], [[16, 8]], 1, -1), e_io)
-        inc(g.iota(T.ib[:, 8:40], [[16, 8], [0, 4]], 1, -1), e_io)
-    if me == 11:
-        inc(g.iota(T.iblk[:], [[16, 8], [0, 16]], 15, -1), e_io)
-        inc(g.iota(T.ir[:, 0:16], [[0, 2], [16, 8]], 15, -1), e_io)
-        inc(g.iota(T.ir[:, 16:48], [[16, 8], [0, 4]], 15, -1), e_io)
-
-    e_win = ev()
-    e_sa, e_sb, e_pa, e_pb, e_store = ev(), ev(), ev(), ev(), ev()
+        inc(g.iota(T.ib[:, 8:72], [[0, 2], [16, 8], [0, 4]], 1, -1), e_io)
+        if "a" in forms:
+            inc(g.iota(T.iba[:], [[0, 16], [16, 4]], 15, -1), e_io)
+        if "b" in forms:
+            inc(g.iota(T.ibb[:], [[0, 2], [16, 8], [0, 4]], 15, -1), e_io)
+        inc(g.iota(T.ipm[:], [[1, 128]], 128, -1), e_io)
+    e_z, e_win, e_win2, e_store = ev(), ev(), ev(), ev()
+    e_hi, e_bias, e_sp, e_pc = ev(), ev(), ev(), ev()
+    if has_map:
+        wait(V, e_k)
+        inc(V.tensor_scalar(T.qi[:], T.kcol[:], 6, None, SHR), e_hi)
+        wait(V, e_hi)
+        inc(V.tensor_scalar(T.bias[:], T.qi[:], -256.0, None, MUL), e_bias)
     if walk:
-        inc(V.memset(T.win[:, 0:4096], 0.0), e_win)
+        inc(V.memset(T.win[:, 0:2048], 0.0), e_z)
+    if two:
+        wait(S, e_z)
+        inc(S.activation(T.win[:, 6144:8192], T.win[:, 0:2048], COPY), e_win)
+        wait(S, e_tab[0])
+        inc(S.activation(T.win2[:, 5120:8192], T.tabs[:, 0:3072], COPY), e_win2)
     if has_map:
         wait(V, e_bp)
-        inc(V.tensor_scalar(T.spa[:], T.bps[:], 15, None, AND), e_sa)
-        inc(V.tensor_scalar(T.spb[:], T.bps[:], 4, None, SHR), e_sb)
-        wait(V, e_sa)
-        inc(V.tensor_copy(T.pca[:], T.spa[:]), e_pa)
-        wait(V, e_sb)
-        inc(V.tensor_scalar(T.pcb[:], T.spb[:], -256.0, None, ADD), e_pb)
-        wait(Y, e_pa)
-        inc(Y.dma_start(T.mine[0:64, :], T.pca[:]), e_store, 16)
-        wait(S, e_pb)
-        inc(S.dma_start(T.mine[64:128, :], T.pcb[:]), e_store, 16)
-        wait(g, e_store)
+        inc(V.tensor_scalar(T.sp[0:64, :], T.bps[0:64, :], 15, None, AND), e_sp)
+        inc(V.tensor_scalar(T.sp[64:128, :], T.bps[64:128, :], 4, None, SHR), e_sp)
+        wait(V, e_sp, e_bias)
+        inc(V.tensor_scalar(T.pc[:], T.sp[:], T.bias[:, 0:1], None, ADD), e_pc)
+        wait(g, e_pc)
         r = SLOT[me]
         for dsts in MAPS_TO[me]:
-            send(dsts, T.land[128 * r:128 * r + 128, :], T.mine[:], "arr%d" % r, "sentm")
-    if walk:
-        inc(V.memset(T.win[:, 4096:8192], 0.0), e_win)
+            send(dsts, T.land[128 * r:128 * r + 128, :], T.pc[:], "arr%d" % r, "sentm")
+        if own:
+            wait(Y, e_pc)
+            inc(Y.dma_start(T.mine[:], T.pc[:]), e_store, 16)
+    if two:
+        inc(V.memset(T.win[:, 2048:6144], 0.0), e_win)
+        inc(V.memset(T.win2[:, 0:5120], 0.0), e_win2)
+    elif walk:
+        inc(V.memset(T.win[:, 2048:8192], 0.0), e_win)
 
     e_c1, e_c2, e_c3 = ev(), ev(), ev()
     rows = {"a": 64, "b": 128}
-    if walk or me == 11:
-        wait(V, e_io)
-        inc(V.tensor_scalar(T.jpm[:], T.ipm[:], 15, None, AND), e_c1)
-        for f in sorted(forms):
+    base = {m: 2 if two and SLOT[m] >= 2 else 0 for m in walk}
+    if walk:
+        wait(V, e_k, e_io)
+        inc(V.tensor_scalar(T.kpar[:], T.kcol[:], 1, None, AND), e_c1)
+        inc(V.tensor_scalar(T.ja[:], T.ia[:], 1, None, SHR), e_c1)
+        inc(V.tensor_scalar(T.jb[:], T.ib[:], 1, None, SHR), e_c1)
+        for f in forms:
             inc(V.tensor_scalar(T["jb" + f][:], T["ib" + f][:], 4, None, SHR), e_c1)
-        if walk:
-            inc(V.tensor_scalar(T.kpar[:], T.kcol[:], 1, None, AND), e_c1)
-            inc(V.tensor_scalar(T.ja[:], T.ia[:], 1, None, SHR), e_c1)
-            inc(V.tensor_scalar(T.jb[:], T.ib[:], 1, None, SHR), e_c1)
-        else:
-            inc(V.tensor_scalar(T.qi[:], T.kcol[:], 15, None, AND), e_c1)
-            inc(V.tensor_scalar(T.jblk[:], T.iblk[:], 4, None, SHR), e_c1)
-            inc(V.tensor_scalar(T.jr[:], T.ir[:], 4, None, SHR), e_c1)
+        inc(V.tensor_scalar(T.jpm[:], T.ipm[:], 15, None, AND), e_c1)
         wait(V, e_c1)
-        if walk:
-            inc(V.tensor_scalar(T.wlist[:], T.kpar[:], -511.0, 512.0, MUL, ADD), e_c2)
-            inc(V.tensor_scalar(T.wnat[:], T.kpar[:], 15.0, 1.0, MUL, ADD), e_c2)
-        else:
-            inc(V.tensor_copy(T.qcol[:], T.qi[:]), e_c2)
-            inc(V.tensor_scalar(T.blk[:], T.jblk[:], 0.0, None, EQ), e_c2)
-            inc(V.tensor_scalar(T.e16[:], T.jpm[:, 0:16], 0.0, None, EQ), e_c2)
-            inc(V.tensor_scalar(T.r11[:, 0:8], T.jr[:, 0:8], 0.0, None, EQ), e_c2)
-            inc(V.tensor_scalar(T.r11[:, 8:16], T.jr[:, 8:16], 0.0, 512.0, EQ, MUL), e_c2)
-            inc(V.tensor_scalar(T.r11[:, 16:48], T.jr[:, 16:48], 0.0, None, EQ), e_c2)
-        inc(V.tensor_scalar(T.pm[:], T.jpm[:], 0.0, None, EQ), e_c3)
-        for f in sorted(forms):
+        inc(V.tensor_scalar(T.wt[:, 0:1], T.kpar[:], -511.0, 512.0, MUL, ADD), e_c2)
+        inc(V.tensor_scalar(T.wt[:, 1:2], T.kpar[:], -1.0, 1.0, MUL, ADD), e_c2)
+        inc(V.tensor_copy(T.wt[:, 2:3], T.kpar[:]), e_c2)
+        inc(V.tensor_scalar(T.pmb[:], T.jpm[:], 0.0, None, EQ), e_c3)
+        inc(V.tensor_scalar(T.pmh[:], T.jpm[:], 0.0, 16.0, EQ, MUL), e_c3)
+        for f in forms:
             inc(V.tensor_scalar(T["bm" + f][:], T["jb" + f][:], 0.0, None, EQ), e_c3)
         wait(V, e_c2)
-    if walk:
         for t, m in enumerate(walk):
-            j, w, n = (T.ja, 4, 36) if m % 2 == 0 else (T.jb, 8, 40)
-            r = SLOT[m]
-            inc(V.tensor_scalar(T.rw[:, 40 * t:40 * t + w], j[:, 0:w], float(-r), T.wlist[:, 0:1], EQ, MUL), e_c3)
+            j, w = (T.ja, 4) if m % 2 == 0 else (T.jb, 8)
+            cols = [(0, w, 0)]
             if t in fin:
-                inc(V.tensor_scalar(T.rw[:, 40 * t + w:40 * t + n], j[:, w:n], float(-r), T.wnat[:, 0:1], EQ, MUL), e_c3)
+                cols += [(w, w + 32, 1), (w + 32, w + 64, 2)]
+            for a, b, i in cols:
+                inc(V.tensor_scalar(T.rw[:, 80 * t + a:80 * t + b], j[:, a:b], float(base[m] - SLOT[m]), T.wt[:, i:i + 1],
+                                    EQ, MUL), e_c3)
             if m % 2:
                 inc(V.memset(T.off_a[64:128, 8 * t:8 * t + 8], 0), e_c3)
 
-    e_wdma = ev()
+    e_wdma, e_wdma2 = ev(), ev()
     if has_map and TAB_MID.get(me):
         Y.wait_ge(T.sem.sentm, sent["sentm"])
         tab_load(TAB_MID[me])
 
-    def fill(q, gp, r0, r1, src):
-        inc(q.dma_start(T.win[16 * gp + 2 * r0:16 * gp + 2 * r1, :], src), e_wdma, 16)
+    def fill(q, gp, s0, s1, src):
+        if two and s0 >= 2:
+            o, w, e = 2, T.win2, e_wdma2
+        else:
+            o, w, e = 0, T.win, e_wdma
+        inc(q.dma_start(w[16 * gp + 2 * (s0 - o):16 * gp + 2 * (s1 - o), :], src), e, 16)
 
     def groups_of(m):
         return range(8) if m % 2 else range(4)
 
-    if walk:
-        wait(Y, e_win)
-        wait(S, e_win)
-        if own:
-            wait(Y, e_store)
-            wait(S, e_store)
-            for gp in groups_of(me):
-                fill((Y, S)[gp % 2], gp, SLOT[me], SLOT[me] + 1, T.mine[:])
-        got = [m for m in walk if m != me]
+    def fill_mine(qs):
+        for q in qs:
+            wait(q, e_store)
+        for gp in groups_of(me):
+            fill(qs[gp % len(qs)], gp, SLOT[me], SLOT[me] + 1, T.mine[:])
+
+    def fill_got(got, qs):
         for m in got:
-            for q in (Y, S):
+            for q in qs:
                 q.wait_ge(T.sem["arr%d" % SLOT[m]], arrived(m))
         for gp in range(8):
             rs = sorted(SLOT[m] for m in got if gp in groups_of(m))
@@ -264,25 +216,28 @@ def rank_program(g, core, T, topo):
                 k = i
                 while k + 1 < len(rs) and rs[k + 1] == rs[k] + 1:
                     k += 1
-                fill((Y, S)[gp % 2], gp, rs[i], rs[k] + 1, T.land[128 * rs[i]:128 * (rs[k] + 1), :])
+                fill(qs[gp % len(qs)], gp, rs[i], rs[k] + 1, T.land[128 * rs[i]:128 * (rs[k] + 1), :])
                 i = k + 1
-    if me not in LIST_TO:
+
+    if me == 9:
+        wait(Y, e_win, e_z)
+        fill_mine((Y,))
+        fill_got([10], (Y,))
+    elif walk:
+        wait(Y, e_win, e_z)
+        wait(S, e_win, e_z)
+        fill_got([10, 9] if two else walk, (Y, S))
+    if two:
+        wait(Y, e_win2)
+        wait(S, e_win2)
+        fill_got([m for m in (7, 8, 6) if m != me], (Y, S))
+        if me == 6:
+            fill_mine((Y, S))
+    if me != 11:
         tab_load(8)
 
-    def finalize(i, t, w, f, addend):
-        k = rows[f]
-        x, pf = T.xf[0:k, 32 * i:32 * i + 32], T.pf[:, 512 * i:512 * i + 32]
-        e1, e2, e3 = ev(), ev(), ev()
-        wait(V, e_c3)
-        inc(V.tensor_tensor(x, T.ps[0:k, 512 * t + w:512 * t + w + 32], T["bm" + f][0:k, :], MUL), e1)
-        wait(PE, e_c3, e1)
-        inc(PE.matmul(pf, T.pm[0:k, :], x, True, True), e2)
-        wait(V, e2)
-        inc(V.tensor_scalar(T.of[:, 32 * i:32 * i + 32], pf, addend, None, ADD), e3)
-        return (T.of, 32 * i), e3
-
     offs = None
-    e_offs = None
+    e_offs = []
     if walk:
         up = 11 if first else (9 if me <= 2 else 6)
         off, c0 = (T.lsta if first else T.lstb), 0
@@ -293,21 +248,22 @@ def rank_program(g, core, T, topo):
         for t, m in enumerate(walk):
             x = 128 * t
             even = m % 2 == 0
-            w, k, n = (4, 128, 36) if even else (8, 64, 40)
-            if t not in fin:
-                n = w
+            w, k = (4, 128) if even else (8, 64)
+            n = w + 64 if t in fin else w
+            h = k // 2
+            win = T.win2 if base[m] else T.win
             e_g, e_s, e_m = ev(), ev(), ev()
-            for q in ((V, S) if even else (V,)):
+            for q in (V, S):
+                if base[m] and not base[walk[t - 1]]:
+                    wait(q, e_wdma2)
                 if e_off is None:
                     q.wait_ge(T.sem.larr, arrived(up))
                 else:
                     wait(q, e_off)
-            inc(V.tensor_copy(T.gat[:, x:x + 64], T.win[:, :].indirect(off[:, c0:c0 + 4])), e_g)
-            if even:
-                inc(S.activation(T.gat[:, x + 64:x + 128], T.win[:, :].indirect(off[:, c0 + 4:c0 + 8]),
-                                 ActivationFunctionType.Copy), e_s)
+            inc(V.tensor_copy(T.gat[:, x:x + h], win[:, :].indirect(off[:, c0:c0 + h // 16])), e_g)
+            inc(S.activation(T.gat[:, x + h:x + k], win[:, :].indirect(off[:, c0 + h // 16:c0 + k // 16]), COPY), e_s)
             wait(PE, e_g, e_s)
-            inc(PE.matmul(T.ps[0:k, 512 * t:512 * t + n], T.gat[:, x:x + k], T.rw[:, 40 * t:40 * t + n], True, True), e_m)
+            inc(PE.matmul(T.ps[0:k, 512 * t:512 * t + n], T.gat[:, x:x + k], T.rw[:, 80 * t:80 * t + n], True, True), e_m)
             wait(V, e_m)
             if t < len(walk) - 1 or me in LIST_TO:
                 off, c0 = (T.off_b, 4 * t) if even else (T.off_a, 8 * t)
@@ -318,15 +274,38 @@ def rank_program(g, core, T, topo):
             for dsts in LIST_TO[me]:
                 send(dsts, T.lstb[:], off[:, c0:c0 + 4], "larr", "sentl")
         for i, t in enumerate(fin):
-            even = walk[t] % 2 == 0
-            o, e = finalize(i, t, 4 if even else 8, "b" if even else "a", 4096.0)
+            w, f = (4, "b") if walk[t] % 2 == 0 else (8, "a")
+            k = rows[f]
+            x, pf = T.xb[0:k, 64 * i:64 * i + 64], T.pf[:, 512 * i:512 * i + 32]
+            e1, e2, e3 = ev(), ev(), ev()
+            inc(V.tensor_tensor(x, T.ps[0:k, 512 * t + w:512 * t + w + 64], T["bm" + f][0:k, :], MUL), e1)
+            wait(PE, e1)
+            PE.matmul(pf, T.pmb[0:k, :], T.xb[0:k, 64 * i:64 * i + 32], True, False)
+            inc(PE.matmul(pf, T.pmh[0:k, :], T.xb[0:k, 64 * i + 32:64 * i + 64], False, True), e2)
+            wait(V, e2)
+            inc(V.tensor_scalar(T.of[:, 32 * i:32 * i + 32], pf, 4096.0, None, ADD), e3)
             if me == 6 and i == 0:
-                wait(g, e)
-                send([OFFS_TO[me]], T.ofl[:], o[0][:, o[1]:o[1] + 32], "oarr", "sentl")
+                wait(g, e3)
+                send([OFFS_TO[me]], T.ofl[:], T.of[:, 0:32], "oarr", "sentl")
             else:
-                offs, e_offs = o, e
+                offs, e_offs = (T.of, 32 * i), [e3]
 
     if me == 11:
+        a1, a2, a3, a4 = ev(), ev(), ev(), ev()
+        inc(g.iota(T.kcol[:], [[0, 1]], 0, 1), a1)
+        inc(g.iota(T.iblk[:], [[16, 8], [0, 16]], 15, -1), a1)
+        inc(g.iota(T.ipm[:], [[1, 128]], 128, -1), a1)
+        inc(g.iota(T.ir[:, 0:16], [[0, 2], [16, 8]], 15, -1), a2)
+        inc(g.iota(T.ir[:, 16:48], [[16, 8], [0, 4]], 15, -1), a2)
+        inc(g.iota(T.iba[:, 0:32], [[0, 8], [16, 4]], 15, -1), a2)
+        wait(V, a1)
+        inc(V.tensor_scalar(T.qi[:], T.kcol[:], 15, None, AND), a3)
+        inc(V.tensor_scalar(T.jblk[:], T.iblk[:], 4, None, SHR), a3)
+        inc(V.tensor_scalar(T.jpm[:], T.ipm[:], 15, None, AND), a3)
+        wait(V, a3)
+        inc(V.tensor_copy(T.qcol[:], T.qi[:]), a4)
+        inc(V.tensor_scalar(T.blk[:], T.jblk[:], 0.0, None, EQ), a4)
+        inc(V.tensor_scalar(T.e16[:], T.jpm[:, 0:16], 0.0, None, EQ), a4)
         e1, e2, e3, e4, e5, e6, e7 = ev(), ev(), ev(), ev(), ev(), ev(), ev()
         wait(V, e_st)
         inc(V.tensor_scalar(T.w0l[:], T.w0[:], 15, None, AND), e1)
@@ -335,18 +314,29 @@ def rank_program(g, core, T, topo):
         inc(V.tensor_copy(T.low[:], T.w0l[:]), e3)
         wait(V, e2)
         inc(V.tensor_copy(T.off0[:], T.w0h[:]), e4)
-        wait(V, e3)
-        for c in range(4):
-            inc(V.tensor_scalar(T.xl[:, 16 * c:16 * c + 16], T.e16[:], T.low[:, c:c + 1], None, MUL), e5)
-        wait(PE, e_c2, e5)
+        for q, cs in ((V, (0, 1)), (S, (2, 3))):
+            wait(q, a4, e3)
+            for c in cs:
+                if q is V:
+                    inc(V.tensor_scalar(T.xl[:, 16 * c:16 * c + 16], T.e16[:], T.low[:, c:c + 1], None, MUL), e5)
+                else:
+                    inc(S.activation(T.xl[:, 16 * c:16 * c + 16], T.e16[:], COPY, scale=T.low[:, c:c + 1]), e5)
+        wait(PE, a4, e5)
         inc(PE.matmul(T.ps[:, 512:576], T.blk[:], T.xl[:], True, True), e6)
+        b1, b2, b3, h0 = ev(), ev(), ev(), ev()
+        wait(V, a2)
+        inc(V.tensor_scalar(T.jr[:], T.ir[:], 4, None, SHR), b1)
         wait(V, e6)
         inc(V.tensor_scalar(T.mask[:], T.ps[:, 512:576], T.qcol[:, 0:1], None, EQ), e7)
-        h0, h1, h2, h3, h4, h5, h6 = ev(), ev(), ev(), ev(), ev(), ev(), ev()
+        wait(V, b1)
+        inc(V.tensor_scalar(T.r11[:, 0:8], T.jr[:, 0:8], 0.0, None, EQ), b2)
+        inc(V.tensor_scalar(T.r11[:, 8:16], T.jr[:, 8:16], 0.0, 512.0, EQ, MUL), b2)
+        inc(V.tensor_scalar(T.r11[:, 16:48], T.jr[:, 16:48], 0.0, None, EQ), b2)
         inc(V.memset(T.off_a[64:128, 0:8], 0), h0)
+        h1, h2, h3, h4, h5, h6 = ev(), ev(), ev(), ev(), ev(), ev()
         wait(V, e7, e4, e_bpw)
         inc(V.tensor_tensor(T.m11[:], T.bpw[:, :].indirect(T.off0[:, 0:4]), T.mask[:], MUL), h1)
-        wait(PE, h1)
+        wait(PE, b2, h1)
         inc(PE.matmul(T.ps[0:64, 0:48], T.m11[:], T.r11[:], True, True), h2)
         wait(V, h2)
         inc(V.tensor_scalar(T.bq[0:64, :], T.ps[0:64, 0:8], 0.0625, -0.46875, MUL, ADD), h3)
@@ -359,28 +349,35 @@ def rank_program(g, core, T, topo):
         wait(g, h0, h6)
         for dsts in LIST_TO[me]:
             send(dsts, T.lsta[:], T.off_a[:, 0:8], "larr", "sentl")
-        o, e = finalize(0, 0, 16, "a", 0.0)
-        wait(g, e)
-        send([OFFS_TO[me]], T.ofl[:], o[0][:, o[1]:o[1] + 32], "oarr", "sentl")
-        k1, k2, k3 = ev(), ev(), ev()
+        k0, k1, k2, k3, k4, k5, k6 = ev(), ev(), ev(), ev(), ev(), ev(), ev()
+        inc(V.tensor_scalar(T.jba[:, 0:32], T.iba[:, 0:32], 4, None, SHR), k0)
+        inc(V.tensor_scalar(T.pm[:], T.jpm[:], 0.0, None, EQ), b3)
+        wait(V, k0)
+        inc(V.tensor_scalar(T.bma[:, 0:32], T.jba[:, 0:32], 0.0, None, EQ), k1)
+        wait(V, k1)
+        inc(V.tensor_tensor(T.xf[0:64, :], T.ps[0:64, 16:48], T.bma[0:64, 0:32], MUL), k2)
+        wait(PE, b3, k2)
+        inc(PE.matmul(T.pf[:, 0:32], T.pm[0:64, :], T.xf[0:64, :], True, True), k3)
+        wait(V, k3)
+        inc(V.tensor_copy(T.of[:, 0:32], T.pf[:, 0:32]), k4)
+        wait(g, k4)
+        send([OFFS_TO[me]], T.ofl[:], T.of[:, 0:32], "oarr", "sentl")
         wait(V, e_st16)
-        inc(V.tensor_copy(T.stf[:], T.st16[:]), k1)
-        wait(PE, k1)
-        inc(PE.matmul(T.pf[:, 512:544], T.pm[0:16, :], T.stf[:], True, True), k2)
-        wait(V, k2)
-        inc(V.tensor_copy(T.of[:, 32:64], T.pf[:, 512:544]), k3)
-        offs, e_offs = (T.of, 32), k3
-
-    if me in LIST_TO:
+        inc(V.tensor_copy(T.stf[:], T.st16[:]), k5)
+        wait(PE, k5)
+        inc(PE.matmul(T.pf[:, 512:544], T.pm[0:16, :], T.stf[:], True, True), k6)
+        e_offs = [ev()]
+        wait(V, k6)
+        inc(V.tensor_copy(T.of[:, 32:64], T.pf[:, 512:544]), e_offs[0])
+        offs = (T.of, 32)
         Y.wait_ge(T.sem.sentl, sent["sentl"])
         tab_load(8)
+
     e_y0, e_y1, e_out = ev(), ev(), ev()
     for q in (V, S):
         if offs is None:
             q.wait_ge(T.sem.oarr, arrived(11 if me == 10 else 6))
-        else:
-            wait(q, e_offs)
-        wait(q, e_tab)
+        wait(q, *(e_offs + e_tab))
     o, c0 = (T.ofl, 0) if offs is None else offs
     inc(V.tensor_copy(T.ysb[:, 0:256], T.tabs[:, :].indirect(o[:, c0:c0 + 16])), e_y0)
     inc(S.activation(T.ysb[:, 256:512], T.tabs[:, :].indirect(o[:, c0 + 16:c0 + 32]),

@@ -1,7 +1,7 @@
 from concourse.bass import DstId, RemoteDMATransfer
 from concourse.mybir import AluOpType, ActivationFunctionType
 
-EQ, MUL, ADD = AluOpType.is_equal, AluOpType.mult, AluOpType.add
+EQ, NE, GE, MUL, ADD = AluOpType.is_equal, AluOpType.not_equal, AluOpType.is_ge, AluOpType.mult, AluOpType.add
 SHR, AND = AluOpType.arith_shift_right, AluOpType.bitwise_and
 COPY = ActivationFunctionType.Copy
 
@@ -10,28 +10,33 @@ def _sb(dt, **cols):
     return {k: ("sbuf", [128, n], dt) for k, n in cols.items()}
 
 
-SCRATCH = {"mine": ("dram", [128, 128], "bfloat16"), "land": ("dram", [640, 128], "bfloat16"),
+SCRATCH = {"mine": ("dram", [128, 128], "bfloat16"), "land": ("dram", [896, 128], "bfloat16"),
            "ps": ("psum", [128, 2560], "float32"), "pf": ("psum", [128, 1024], "float32"),
            "st16": ("sbuf", [16, 32], "int32"), "stf": ("sbuf", [16, 32], "float32")}
-SCRATCH.update(_sb("bfloat16", tabs=8192, win=8192, win2=8192, pc=128, ysb=512, gat=640, rw=400, e16=16, blk=128, xl=64, pmb=128,
-                   pmh=128, xb=128, bma=64, bmb=64))
-SCRATCH.update(_sb("uint16", lsta=8, lstb=4, ofl=32, off_a=40, off_b=20, of=64, off0=4))
-SCRATCH.update(_sb("int32", bps=128, sp=128, kcol=1, kpar=1, ia=68, ja=68, ib=72, jb=72, iba=64, jba=64, ibb=64, jbb=64,
-                   ipm=128, jpm=128, bpw=512, w0=4, w0h=4, w0l=4, qi=1, iblk=128, jblk=128, ir=48, jr=48, bq=8))
-SCRATCH.update(_sb("float32", xf=32, wt=3, bias=1, pm=128, low=4, qcol=1, r11=48, mask=64, m11=64, tq=8, oq=8))
+SCRATCH.update(_sb("bfloat16", tabs=8192, win=8192, win2=8192, cmp0=1024, cmp1=1024, pc=128, ysb=512, gat=640, rwm=56, rwf=128,
+                   one=128, e16=16, blk=128, xl=64, pmb=128, xb=128, bma=64, bmb=64))
+SCRATCH.update(_sb("uint16", lsta=8, lstb=4, ofl=32, off_a=40, off_b=20, of=64, off0=4, ol=64, l0=64, l1=64))
+SCRATCH.update(_sb("int32", bps=128, sp=128, bpl=64, bl=64, bh=64, bm=64, bo=64, kcol=1, iba=32, jba=32,
+                   ipm=128, jpm=128, bpw=512, w0=4, w0h=4, w0l=4, qi=1, bq=8))
+SCRATCH.update(_sb("float32", xf=32, bias=1, pm=128, low=4, qcol=1, one32=48, r11=48, mask=64, m11=64, tq=8, oq=8))
 
-SEMAPHORES = ["e%d" % _i for _i in range(100)] + ["arr%d" % _i for _i in range(5)] + ["larr", "oarr", "sentm", "sentl"]
+SEMAPHORES = (["e%d" % _i for _i in range(110)] + ["arr%d" % _i for _i in range(7)] +
+              ["lar0", "lar1", "larr", "oarr", "sentm", "sentl"])
 
 WALK = {9: [10, 9, 8, 7, 6], 8: [10, 9], 7: [10, 9, 8], 6: [10, 9, 8, 7, 6],
-        4: [5], 3: [5, 4], 2: [5, 4, 3], 1: [5, 4, 3, 2], 0: [5, 4, 3, 2, 1]}
-SLOT = {9: 0, 10: 1, 7: 2, 8: 3, 6: 4, 5: 0, 3: 1, 1: 2, 4: 3, 2: 4}
-TWO = (9, 6)
-MAPS_TO = {10: [[9], [6, 8, 7]], 9: [[6], [8, 7]], 8: [[9], [6, 7]], 7: [[9], [6]], 6: [[9]],
-           5: [[0], [1, 2, 3, 4]], 4: [[0], [1, 2, 3]], 3: [[0], [1, 2]], 2: [[0], [1]], 1: [[0]]}
+        4: [5], 3: [5, 4], 2: ["5.4", 3], 1: ["5.4", "3.2"], 0: ["5.4", "3.2", 1]}
+FIN = {9: [0], 8: [1], 7: [2], 6: [4, 3], 4: [0], 3: [1], 2: [1], 1: [1], 0: [2]}
+JOIN = {"5.4": (5, 4), "3.2": (3, 2)}
+SLOT = {9: 0, 10: 1, 7: 2, 8: 3, 6: 4, 4: 0, 2: 1, "3.2": 2, "5.4": 3, 1: 4, 3: 5, 5: 6}
+WIN2 = {9: [7, 8, 6], 6: [7, 8, 6], 2: ["5.4", 3], 1: ["5.4"], 0: ["5.4", 1]}
+MAPS_TO = {10: [[9, 6], [8, 7]], 9: [[6], [8, 7]], 8: [[7], [9, 6]], 7: [[9], [6]], 6: [[9]],
+           5: [[3, 4]], 4: [[0], [1, 2, 3]], 3: [[2]], 2: [[0], [1]], 1: [[0]]}
+ENTRIES_TO = {5: ("l0", "lar0", [[0], [1, 2]]), 3: ("l1", "lar1", [[0], [1]])}
 LIST_TO = {11: [[9], [6, 7, 8]], 9: [[0], [1, 2]], 6: [[3, 4]]}
 OFFS_TO = {11: 10, 6: 5}
-TAB_EARLY = {11: 3, 10: 2, 9: 3, 8: 2, 7: 2, 6: 3, 0: 6}
-TAB_MID = {10: 6, 6: 2, 5: 4}
+TAB_EARLY = {11: 3, 10: 2, 9: 5, 8: 2, 7: 2, 6: 5, 0: 8, 1: 6, 2: 4.5}
+TAB_MID = {10: 6, 5: 4}
+FILLER = {9: 768}
 
 
 def rank_program(g, core, T, topo):
@@ -78,23 +83,33 @@ def rank_program(g, core, T, topo):
     has_map = 1 <= me <= 10
     own = me in walk
     first = walk[:1] == [10]
-    two = me in TWO
+    two = me in WIN2
+    in2 = WIN2.get(me, [])
+    joins = [m for m in walk if m in JOIN]
+    last = len(walk) - 1
+    wide = [(t % 2 == 1) if first else (t % 2 == 0) for t in range(len(walk))]
+    fin = FIN.get(me, [])
+    forms = sorted(set("a" if wide[t] else "b" for t in fin))
 
     e_tab = []
     tab_at = [0]
 
     def tab_load(units):
         a = tab_at[0]
-        b = min(8192, a + 1024 * units)
+        b = min(8192, a + int(1024 * units))
         if b > a:
             e_tab.append(ev())
             inc(Y.dma_start(T.tabs[:, a:b], T.tab[:, a:b]), e_tab[-1], 16)
         tab_at[0] = b
 
-    e_bp, e_st, e_bpw, e_st16 = ev(), ev(), ev(), ev()
+    e_bp, e_st, e_bpw, e_st16, e_bpl, e_fil = ev(), ev(), ev(), ev(), ev(), ev()
     if has_map:
         inc(Y.dma_start(T.bps[0:64, :], T.bp[:]), e_bp, 16)
         inc(S.dma_start(T.bps[64:128, :], T.bp[:]), e_bp, 16)
+    if me in ENTRIES_TO:
+        for k in range(8):
+            q = (Y, S)[k % 2]
+            inc(q.dma_start(T.bpl[16 * k:16 * k + 16, :], T.bp[:, 64 * k:64 * k + 64]), e_bpl, 16)
     if me == 11:
         for q, gs in ((Y, (0, 1, 2, 3)), (S, (4, 5, 6, 7))):
             for k in gs:
@@ -102,38 +117,24 @@ def rank_program(g, core, T, topo):
             for k in gs:
                 inc(q.dma_start(T.bpw[16 * k:16 * k + 16, :], T.bp[:]), e_bpw, 16)
         inc(Y.dma_start(T.st16[:], T.st[:]), e_st16, 16)
+    if me in FILLER:
+        inc(S.dma_start(T.win2[:, 8192 - FILLER[me]:8192], T.tab[:, 0:FILLER[me]]), e_fil, 16)
     tab_load(TAB_EARLY.get(me, 4))
 
-    fin = []
-    if walk:
-        fin = [len(walk) - 1, walk.index(7)] if me == 6 else [walk.index(me + 1)]
-    forms = sorted(set("b" if walk[t] % 2 == 0 else "a" for t in fin))
-    e_k, e_io = ev(), ev()
-    if me != 11:
-        inc(g.iota(T.kcol[:], [[0, 1]], 0, 1), e_k)
-    if walk:
-        inc(g.iota(T.ia[:], [[0, 17], [16, 4]], 1, -1), e_io)
-        inc(g.iota(T.ib[:, 0:8], [[16, 8]], 1, -1), e_io)
-        inc(g.iota(T.ib[:, 8:72], [[0, 2], [16, 8], [0, 4]], 1, -1), e_io)
-        if "a" in forms:
-            inc(g.iota(T.iba[:], [[0, 16], [16, 4]], 15, -1), e_io)
-        if "b" in forms:
-            inc(g.iota(T.ibb[:], [[0, 2], [16, 8], [0, 4]], 15, -1), e_io)
-        inc(g.iota(T.ipm[:], [[1, 128]], 128, -1), e_io)
-    e_z, e_win, e_win2, e_store = ev(), ev(), ev(), ev()
-    e_hi, e_bias, e_sp, e_pc = ev(), ev(), ev(), ev()
+    e_one, e_z, e_win, e_win2, e_store, h0 = ev(), ev(), ev(), ev(), ev(), ev()
+    e_bias, e_sp, e_pc, e_io = ev(), ev(), ev(), ev()
     if has_map:
-        wait(V, e_k)
-        inc(V.tensor_scalar(T.qi[:], T.kcol[:], 6, None, SHR), e_hi)
-        wait(V, e_hi)
-        inc(V.tensor_scalar(T.bias[:], T.qi[:], -256.0, None, MUL), e_bias)
+        inc(V.memset(T.bias[0:64, :], 0.0), e_bias)
+        inc(V.memset(T.bias[64:128, :], -256.0), e_bias)
     if walk:
-        inc(V.memset(T.win[:, 0:2048], 0.0), e_z)
+        inc(V.memset((T.win2 if two else T.win)[:, 0:2048], 0.0), e_z)
     if two:
         wait(S, e_z)
-        inc(S.activation(T.win[:, 6144:8192], T.win[:, 0:2048], COPY), e_win)
-        wait(S, e_tab[0])
-        inc(S.activation(T.win2[:, 5120:8192], T.tabs[:, 0:3072], COPY), e_win2)
+        inc(S.activation(T.win[:, 6144:8192], T.win2[:, 0:2048], COPY), e_win)
+        inc(S.activation(T.win2[:, 4608:6656], T.win2[:, 0:2048], COPY), e_win2)
+        if not joins:
+            n = 1536 - FILLER.get(me, 0)
+            inc(S.activation(T.win2[:, 6656:6656 + n], T.win2[:, 0:n], COPY), e_win2)
     if has_map:
         wait(V, e_bp)
         inc(V.tensor_scalar(T.sp[0:64, :], T.bps[0:64, :], 15, None, AND), e_sp)
@@ -147,63 +148,97 @@ def rank_program(g, core, T, topo):
         if own:
             wait(Y, e_pc)
             inc(Y.dma_start(T.mine[:], T.pc[:]), e_store, 16)
+    if me in ENTRIES_TO:
+        x1, x2, x3, x4 = ev(), ev(), ev(), ev()
+        wait(V, e_bpl)
+        inc(V.tensor_scalar(T.bl[:], T.bpl[:], 15, None, AND), x1)
+        inc(V.tensor_scalar(T.bh[:], T.bpl[:], 4, None, SHR), x2)
+        wait(V, x1)
+        inc(V.tensor_scalar(T.bm[:], T.bl[:], 512.0, None, MUL), x2)
+        wait(V, x2)
+        inc(V.tensor_tensor(T.bo[:], T.bm[:], T.bh[:], ADD), x3)
+        wait(V, x3)
+        inc(V.tensor_copy(T.ol[:], T.bo[:]), x4)
+        wait(g, x4)
+        buf, sm, calls = ENTRIES_TO[me]
+        for dsts in calls:
+            send(dsts, T[buf][:], T.ol[:], sm, "sentm")
+    if walk:
+        inc(V.memset(T.one[:, 0:64], 1.0), e_one)
+        inc(V.memset(T.one[:, 64:128], 16.0), e_one)
+        if any(wide[:-1]):
+            inc(V.memset(T.off_a[64:128, :], 0), h0)
     if two:
-        inc(V.memset(T.win[:, 2048:6144], 0.0), e_win)
-        inc(V.memset(T.win2[:, 0:5120], 0.0), e_win2)
+        inc(V.memset(T.win[:, 0:6144], 0.0), e_win)
+        inc(V.memset(T.win2[:, 2048:4608], 0.0), e_win2)
+        if joins:
+            inc(V.memset(T.win2[:, 6656:8192], 0.0), e_win2)
     elif walk:
         inc(V.memset(T.win[:, 2048:8192], 0.0), e_win)
 
-    e_c1, e_c2, e_c3 = ev(), ev(), ev()
-    rows = {"a": 64, "b": 128}
-    base = {m: 2 if two and SLOT[m] >= 2 else 0 for m in walk}
+    e_rw, e_rwf, e_jp, e_pmb, e_bm = ev(), ev(), ev(), ev(), ev()
+
+    def kind(t):
+        if t < last:
+            return "v" if walk[t + 1] in JOIN else "o"
+        if me in LIST_TO:
+            return "v" if WALK[LIST_TO[me][0][0]][0] in JOIN else "o"
+        return None
+
     if walk:
-        wait(V, e_k, e_io)
-        inc(V.tensor_scalar(T.kpar[:], T.kcol[:], 1, None, AND), e_c1)
-        inc(V.tensor_scalar(T.ja[:], T.ia[:], 1, None, SHR), e_c1)
-        inc(V.tensor_scalar(T.jb[:], T.ib[:], 1, None, SHR), e_c1)
+        wait(g, e_one)
+        todo = sorted((SLOT[walk[t]], kind(t)) for t in range(len(walk)) if kind(t))
+        runs = []
+        for s, k in todo:
+            if runs and runs[-1][2] == k and runs[-1][0] + runs[-1][1] == s:
+                runs[-1][1] += 1
+            else:
+                runs.append([s, 1, k])
+        e_r0 = ev()
+        for s, n, k in runs:
+            out, one = T.rwm[:, 8 * s:8 * (s + n)], T.one[:, 0:8 * n]
+            inc(g.affine_select(out, one, [[-2, n], [-16, 8]], EQ, 0.0, -2 * s - (1 if k == "o" else 0), 1), e_r0)
+        wait(g, e_r0)
+        for s, n, k in runs:
+            out = T.rwm[:, 8 * s:8 * (s + n)]
+            inc(g.affine_select(out, out, [[-2, n], [-16, 8]], NE, 512.0 if k == "o" else 16.0,
+                                -2 * s - (0 if k == "o" else 1), 1), e_rw)
+        inc(g.iota(T.ipm[:], [[1, 128]], 128, -1), e_io)
+        for i, t in enumerate(fin):
+            pat = [[-16, 8], [0, 4]] if wide[t] else [[0, 8], [-16, 4]]
+            s = SLOT[walk[t]]
+            inc(g.affine_select(T.rwf[:, 64 * i:64 * i + 32], T.one[:, 0:32], pat, EQ, 0.0, -2 * s, 1), e_rwf)
+            inc(g.affine_select(T.rwf[:, 64 * i + 32:64 * i + 64], T.one[:, 64:96], pat, EQ, 0.0, -2 * s - 1, 1), e_rwf)
+        e_b0 = ev()
+        pats = {"a": ([[0, 16], [-16, 4]], [[0, 16], [16, 4]]), "b": ([[0, 2], [-16, 8], [0, 4]], [[0, 2], [16, 8], [0, 4]])}
         for f in forms:
-            inc(V.tensor_scalar(T["jb" + f][:], T["ib" + f][:], 4, None, SHR), e_c1)
-        inc(V.tensor_scalar(T.jpm[:], T.ipm[:], 15, None, AND), e_c1)
-        wait(V, e_c1)
-        inc(V.tensor_scalar(T.wt[:, 0:1], T.kpar[:], -511.0, 512.0, MUL, ADD), e_c2)
-        inc(V.tensor_scalar(T.wt[:, 1:2], T.kpar[:], -1.0, 1.0, MUL, ADD), e_c2)
-        inc(V.tensor_copy(T.wt[:, 2:3], T.kpar[:]), e_c2)
-        inc(V.tensor_scalar(T.pmb[:], T.jpm[:], 0.0, None, EQ), e_c3)
-        inc(V.tensor_scalar(T.pmh[:], T.jpm[:], 0.0, 16.0, EQ, MUL), e_c3)
+            b = T["bm" + f]
+            inc(g.affine_select(b[:], T.one[:, 0:64], pats[f][0], GE, 0.0, 0, 1), e_b0)
+        wait(g, e_b0)
         for f in forms:
-            inc(V.tensor_scalar(T["bm" + f][:], T["jb" + f][:], 0.0, None, EQ), e_c3)
-        wait(V, e_c2)
-        for t, m in enumerate(walk):
-            j, w = (T.ja, 4) if m % 2 == 0 else (T.jb, 8)
-            cols = [(0, w, 0)]
-            if t in fin:
-                cols += [(w, w + 32, 1), (w + 32, w + 64, 2)]
-            for a, b, i in cols:
-                inc(V.tensor_scalar(T.rw[:, 80 * t + a:80 * t + b], j[:, a:b], float(base[m] - SLOT[m]), T.wt[:, i:i + 1],
-                                    EQ, MUL), e_c3)
-            if m % 2:
-                inc(V.memset(T.off_a[64:128, 8 * t:8 * t + 8], 0), e_c3)
+            b = T["bm" + f]
+            inc(g.affine_select(b[:], b[:], pats[f][1], GE, 0.0, 15, -1), e_bm)
+        wait(V, e_io)
+        inc(V.tensor_scalar(T.jpm[:], T.ipm[:], 15, None, AND), e_jp)
+        wait(V, e_jp)
+        inc(V.tensor_scalar(T.pmb[:], T.jpm[:], 0.0, None, EQ), e_pmb)
 
     e_wdma, e_wdma2 = ev(), ev()
     if has_map and TAB_MID.get(me):
         Y.wait_ge(T.sem.sentm, sent["sentm"])
         tab_load(TAB_MID[me])
 
-    def fill(q, gp, s0, s1, src):
-        if two and s0 >= 2:
-            o, w, e = 2, T.win2, e_wdma2
-        else:
-            o, w, e = 0, T.win, e_wdma
-        inc(q.dma_start(w[16 * gp + 2 * (s0 - o):16 * gp + 2 * (s1 - o), :], src), e, 16)
+    def fill(q, gp, s0, s1, src, second):
+        w, e = (T.win2, e_wdma2) if second else (T.win, e_wdma)
+        inc(q.dma_start(w[16 * gp + 2 * s0:16 * gp + 2 * s1, :], src), e, 16)
 
     def groups_of(m):
-        return range(8) if m % 2 else range(4)
+        return range(8) if m not in walk or wide[walk.index(m)] else range(4)
 
-    def fill_mine(qs):
-        for q in qs:
-            wait(q, e_store)
+    def fill_mine():
+        wait(Y, e_store)
         for gp in groups_of(me):
-            fill(qs[gp % len(qs)], gp, SLOT[me], SLOT[me] + 1, T.mine[:])
+            fill(Y, gp, SLOT[me], SLOT[me] + 1, T.mine[:], me in in2)
 
     def fill_got(got, qs):
         for m in got:
@@ -216,23 +251,58 @@ def rank_program(g, core, T, topo):
                 k = i
                 while k + 1 < len(rs) and rs[k + 1] == rs[k] + 1:
                     k += 1
-                fill(qs[gp % len(qs)], gp, rs[i], rs[k] + 1, T.land[128 * rs[i]:128 * (rs[k] + 1), :])
+                fill(qs[gp % len(qs)], gp, rs[i], rs[k] + 1, T.land[128 * rs[i]:128 * (rs[k] + 1), :], got[0] in in2)
                 i = k + 1
 
-    if me == 9:
-        wait(Y, e_win, e_z)
-        fill_mine((Y,))
-        fill_got([10], (Y,))
-    elif walk:
-        wait(Y, e_win, e_z)
-        wait(S, e_win, e_z)
-        fill_got([10, 9] if two else walk, (Y, S))
+    if walk:
+        qs = (Y,) if me in LIST_TO else (Y, S)
+        for q in qs:
+            wait(q, e_win, e_z)
+        if joins:
+            fill_got(sorted((JOIN[m][1] for m in joins), reverse=True), qs)
+        elif two:
+            if own and me not in in2:
+                fill_mine()
+            fill_got([m for m in walk if m != me and m not in in2], qs)
+        else:
+            fill_got(walk, qs)
     if two:
-        wait(Y, e_win2)
-        wait(S, e_win2)
-        fill_got([m for m in (7, 8, 6) if m != me], (Y, S))
-        if me == 6:
-            fill_mine((Y, S))
+        rest = [m for m in in2 if m != me and m not in JOIN]
+        if rest:
+            for q in (Y, S):
+                wait(q, e_z, e_win, e_win2, e_fil)
+            fill_got(rest, (Y,) if joins else (Y, S))
+        if own and me in in2:
+            fill_mine()
+
+    e_cp, e_join = [], {}
+    if joins:
+        wait(V, e_wdma)
+        wait(S, e_wdma)
+        for i, m in enumerate(joins):
+            x, y = JOIN[m]
+            e = ev()
+            e_cp.append(e)
+            lst, out = T["l%d" % i], T["cmp%d" % i]
+            for q in (V, S):
+                q.wait_ge(T.sem["lar%d" % i], arrived(x))
+            inc(V.tensor_copy(out[:, 0:512], T.win[:, :].indirect(lst[:, 0:32])), e)
+            inc(S.activation(out[:, 512:1024], T.win[:, :].indirect(lst[:, 32:64]), COPY), e)
+        for i, m in enumerate(joins):
+            qs = (Y,) if i == 0 and len(joins) > 1 else (Y, S)
+            second = m in in2
+            for q in qs:
+                wait(q, *e_cp[0:i + 1])
+                if second:
+                    wait(q, e_win, e_win2)
+            e_join[m] = ev()
+            a, n = 2 * SLOT[JOIN[m][1]], 0
+            for gp in groups_of(m):
+                for k in (0, 1):
+                    o = 16 * gp + 2 * SLOT[m] + k
+                    inc(qs[n % len(qs)].dma_start((T.win2 if second else T.win)[o:o + 1, :], T["cmp%d" % i][a + k:128:16, :]),
+                        e_join[m], 16)
+                    n += 1
     if me != 11:
         tab_load(8)
 
@@ -242,46 +312,56 @@ def rank_program(g, core, T, topo):
         up = 11 if first else (9 if me <= 2 else 6)
         off, c0 = (T.lsta if first else T.lstb), 0
         e_off = None
-        wait(PE, e_c3)
-        wait(V, e_c3, e_wdma)
-        wait(S, e_c3, e_wdma)
+        wait(PE, e_rw)
+        wait(V, h0)
+        seen = []
         for t, m in enumerate(walk):
             x = 128 * t
-            even = m % 2 == 0
-            w, k = (4, 128) if even else (8, 64)
-            n = w + 64 if t in fin else w
+            w, k = (8, 64) if wide[t] else (4, 128)
             h = k // 2
-            win = T.win2 if base[m] else T.win
-            e_g, e_s, e_m = ev(), ev(), ev()
+            win = T.win2 if m in in2 else T.win
+            e_g, e_m = ev(), ev()
+            ready = [e_wdma2, e_win2, e_fil] if m in in2 else [e_wdma, e_win, e_z]
+            ready += [e_join[j] for j in joins if (j in in2) == (m in in2)]
             for q in (V, S):
-                if base[m] and not base[walk[t - 1]]:
-                    wait(q, e_wdma2)
+                if (m in in2) not in seen:
+                    wait(q, *ready)
                 if e_off is None:
                     q.wait_ge(T.sem.larr, arrived(up))
                 else:
                     wait(q, e_off)
+            seen.append(m in in2)
             inc(V.tensor_copy(T.gat[:, x:x + h], win[:, :].indirect(off[:, c0:c0 + h // 16])), e_g)
-            inc(S.activation(T.gat[:, x + h:x + k], win[:, :].indirect(off[:, c0 + h // 16:c0 + k // 16]), COPY), e_s)
-            wait(PE, e_g, e_s)
-            inc(PE.matmul(T.ps[0:k, 512 * t:512 * t + n], T.gat[:, x:x + k], T.rw[:, 80 * t:80 * t + n], True, True), e_m)
-            wait(V, e_m)
-            if t < len(walk) - 1 or me in LIST_TO:
-                off, c0 = (T.off_b, 4 * t) if even else (T.off_a, 8 * t)
+            inc(S.activation(T.gat[:, x + h:x + k], win[:, :].indirect(off[:, c0 + h // 16:c0 + k // 16]), COPY), e_g)
+            wait(PE, e_g)
+            kd = kind(t)
+            if kd:
+                s = 8 * SLOT[m]
+                inc(PE.matmul(T.ps[0:k, 512 * t:512 * t + w], T.gat[:, x:x + k], T.rwm[:, s:s + w], True, True), e_m)
+                wait(V, e_m)
+                off, c0 = (T.off_a, 8 * t) if wide[t] else (T.off_b, 4 * t)
                 e_off = ev()
-                inc(V.tensor_scalar(off[0:k, c0:c0 + w], T.ps[0:k, 512 * t:512 * t + w], 256.0, None, ADD), e_off)
+                inc(V.tensor_scalar(off[0:k, c0:c0 + w], T.ps[0:k, 512 * t:512 * t + w], 256.0 if kd == "o" else 4096.0, None, ADD),
+                    e_off)
         if me in LIST_TO:
             wait(g, e_off)
             for dsts in LIST_TO[me]:
                 send(dsts, T.lstb[:], off[:, c0:c0 + 4], "larr", "sentl")
+        wait(PE, e_rwf, e_pmb)
+        if e_off is not None:
+            wait(PE, e_off)
+        wait(V, e_bm)
         for i, t in enumerate(fin):
-            w, f = (4, "b") if walk[t] % 2 == 0 else (8, "a")
-            k = rows[f]
+            k, f = (64, "a") if wide[t] else (128, "b")
             x, pf = T.xb[0:k, 64 * i:64 * i + 64], T.pf[:, 512 * i:512 * i + 32]
-            e1, e2, e3 = ev(), ev(), ev()
-            inc(V.tensor_tensor(x, T.ps[0:k, 512 * t + w:512 * t + w + 64], T["bm" + f][0:k, :], MUL), e1)
+            pt = T.ps[0:k, 512 * t + 64:512 * t + 128]
+            e0, e1, e2, e3 = ev(), ev(), ev(), ev()
+            inc(PE.matmul(pt, T.gat[:, 128 * t:128 * t + k], T.rwf[:, 64 * i:64 * i + 64], True, True), e0)
+            wait(V, e0)
+            inc(V.tensor_tensor(x, pt, T["bm" + f][0:k, :], MUL), e1)
             wait(PE, e1)
             PE.matmul(pf, T.pmb[0:k, :], T.xb[0:k, 64 * i:64 * i + 32], True, False)
-            inc(PE.matmul(pf, T.pmh[0:k, :], T.xb[0:k, 64 * i + 32:64 * i + 64], False, True), e2)
+            inc(PE.matmul(pf, T.pmb[0:k, :], T.xb[0:k, 64 * i + 32:64 * i + 64], False, True), e2)
             wait(V, e2)
             inc(V.tensor_scalar(T.of[:, 32 * i:32 * i + 32], pf, 4096.0, None, ADD), e3)
             if me == 6 and i == 0:
@@ -291,20 +371,31 @@ def rank_program(g, core, T, topo):
                 offs, e_offs = (T.of, 32 * i), [e3]
 
     if me == 11:
-        a1, a2, a3, a4 = ev(), ev(), ev(), ev()
+        a1, a3, a4, a5, b0, b1, b2, b3 = ev(), ev(), ev(), ev(), ev(), ev(), ev(), ev()
+        inc(V.memset(T.off_a[64:128, 0:8], 0), h0)
+        inc(V.memset(T.one[:], 1.0), b0)
+        inc(V.memset(T.one32[:], 1.0), b1)
+        wait(V, b1)
+        inc(V.memset(T.one32[:, 8:16], 512.0), b2)
         inc(g.iota(T.kcol[:], [[0, 1]], 0, 1), a1)
-        inc(g.iota(T.iblk[:], [[16, 8], [0, 16]], 15, -1), a1)
         inc(g.iota(T.ipm[:], [[1, 128]], 128, -1), a1)
-        inc(g.iota(T.ir[:, 0:16], [[0, 2], [16, 8]], 15, -1), a2)
-        inc(g.iota(T.ir[:, 16:48], [[16, 8], [0, 4]], 15, -1), a2)
-        inc(g.iota(T.iba[:, 0:32], [[0, 8], [16, 4]], 15, -1), a2)
+        c1, c2, c3, c4 = ev(), ev(), ev(), ev()
+        wait(g, b0)
+        inc(g.affine_select(T.blk[:], T.one[:], [[-16, 8], [0, 16]], GE, 0.0, 0, 1), c1)
+        wait(g, c1)
+        inc(g.affine_select(T.blk[:], T.blk[:], [[16, 8], [0, 16]], GE, 0.0, 15, -1), c2)
+        wait(g, b1, b2)
+        inc(g.affine_select(T.r11[:, 0:16], T.one32[:, 0:16], [[0, 2], [-16, 8]], GE, 0.0, 0, 1), c3)
+        inc(g.affine_select(T.r11[:, 16:48], T.one32[:, 16:48], [[-16, 8], [0, 4]], GE, 0.0, 0, 1), c3)
+        wait(g, c3)
+        inc(g.affine_select(T.r11[:, 0:16], T.r11[:, 0:16], [[0, 2], [16, 8]], GE, 0.0, 15, -1), c4)
+        inc(g.affine_select(T.r11[:, 16:48], T.r11[:, 16:48], [[16, 8], [0, 4]], GE, 0.0, 15, -1), c4)
+        inc(g.iota(T.iba[:, 0:32], [[0, 8], [16, 4]], 15, -1), a5)
         wait(V, a1)
         inc(V.tensor_scalar(T.qi[:], T.kcol[:], 15, None, AND), a3)
-        inc(V.tensor_scalar(T.jblk[:], T.iblk[:], 4, None, SHR), a3)
         inc(V.tensor_scalar(T.jpm[:], T.ipm[:], 15, None, AND), a3)
         wait(V, a3)
         inc(V.tensor_copy(T.qcol[:], T.qi[:]), a4)
-        inc(V.tensor_scalar(T.blk[:], T.jblk[:], 0.0, None, EQ), a4)
         inc(V.tensor_scalar(T.e16[:], T.jpm[:, 0:16], 0.0, None, EQ), a4)
         e1, e2, e3, e4, e5, e6, e7 = ev(), ev(), ev(), ev(), ev(), ev(), ev()
         wait(V, e_st)
@@ -312,8 +403,6 @@ def rank_program(g, core, T, topo):
         inc(V.tensor_scalar(T.w0h[:], T.w0[:], 4, None, SHR), e2)
         wait(V, e1)
         inc(V.tensor_copy(T.low[:], T.w0l[:]), e3)
-        wait(V, e2)
-        inc(V.tensor_copy(T.off0[:], T.w0h[:]), e4)
         for q, cs in ((V, (0, 1)), (S, (2, 3))):
             wait(q, a4, e3)
             for c in cs:
@@ -321,22 +410,16 @@ def rank_program(g, core, T, topo):
                     inc(V.tensor_scalar(T.xl[:, 16 * c:16 * c + 16], T.e16[:], T.low[:, c:c + 1], None, MUL), e5)
                 else:
                     inc(S.activation(T.xl[:, 16 * c:16 * c + 16], T.e16[:], COPY, scale=T.low[:, c:c + 1]), e5)
-        wait(PE, a4, e5)
+        wait(V, e2)
+        inc(V.tensor_copy(T.off0[:], T.w0h[:]), e4)
+        wait(PE, c2, e5)
         inc(PE.matmul(T.ps[:, 512:576], T.blk[:], T.xl[:], True, True), e6)
-        b1, b2, b3, h0 = ev(), ev(), ev(), ev()
-        wait(V, a2)
-        inc(V.tensor_scalar(T.jr[:], T.ir[:], 4, None, SHR), b1)
         wait(V, e6)
         inc(V.tensor_scalar(T.mask[:], T.ps[:, 512:576], T.qcol[:, 0:1], None, EQ), e7)
-        wait(V, b1)
-        inc(V.tensor_scalar(T.r11[:, 0:8], T.jr[:, 0:8], 0.0, None, EQ), b2)
-        inc(V.tensor_scalar(T.r11[:, 8:16], T.jr[:, 8:16], 0.0, 512.0, EQ, MUL), b2)
-        inc(V.tensor_scalar(T.r11[:, 16:48], T.jr[:, 16:48], 0.0, None, EQ), b2)
-        inc(V.memset(T.off_a[64:128, 0:8], 0), h0)
         h1, h2, h3, h4, h5, h6 = ev(), ev(), ev(), ev(), ev(), ev()
         wait(V, e7, e4, e_bpw)
         inc(V.tensor_tensor(T.m11[:], T.bpw[:, :].indirect(T.off0[:, 0:4]), T.mask[:], MUL), h1)
-        wait(PE, b2, h1)
+        wait(PE, c4, h1)
         inc(PE.matmul(T.ps[0:64, 0:48], T.m11[:], T.r11[:], True, True), h2)
         wait(V, h2)
         inc(V.tensor_scalar(T.bq[0:64, :], T.ps[0:64, 0:8], 0.0625, -0.46875, MUL, ADD), h3)
@@ -350,6 +433,7 @@ def rank_program(g, core, T, topo):
         for dsts in LIST_TO[me]:
             send(dsts, T.lsta[:], T.off_a[:, 0:8], "larr", "sentl")
         k0, k1, k2, k3, k4, k5, k6 = ev(), ev(), ev(), ev(), ev(), ev(), ev()
+        wait(V, a5)
         inc(V.tensor_scalar(T.jba[:, 0:32], T.iba[:, 0:32], 4, None, SHR), k0)
         inc(V.tensor_scalar(T.pm[:], T.jpm[:], 0.0, None, EQ), b3)
         wait(V, k0)

from concourse.bass import DstId, RemoteDMATransfer
from concourse.mybir import AluOpType, ActivationFunctionType

EQ, NE, GE, MUL, ADD = AluOpType.is_equal, AluOpType.not_equal, AluOpType.is_ge, AluOpType.mult, AluOpType.add
SHR, AND = AluOpType.arith_shift_right, AluOpType.bitwise_and
COPY = ActivationFunctionType.Copy


def _sb(dt, **cols):
    return {k: ("sbuf", [128, n], dt) for k, n in cols.items()}


SCRATCH = {"mine": ("dram", [128, 128], "bfloat16"), "land": ("dram", [896, 128], "bfloat16"),
           "ps": ("psum", [128, 2560], "float32"), "pf": ("psum", [128, 1024], "float32"),
           "st16": ("sbuf", [16, 32], "int32"), "stf": ("sbuf", [16, 32], "float32")}
SCRATCH.update(_sb("bfloat16", tabs=8192, win=8192, win2=8192, cmp0=1024, cmp1=1024, pc=128, ysb=512, gat=640, rwm=56, rwf=128,
                   one=128, e16=16, blk=128, xl=64, pmb=128, xb=128, bma=64, bmb=64))
SCRATCH.update(_sb("uint16", lsta=8, lstb=4, ofl=32, off_a=40, off_b=20, of=64, off0=4, ol=64, l0=64, l1=64))
SCRATCH.update(_sb("int32", bps=128, sp=128, bpl=64, bl=64, bh=64, bm=64, bo=64, kcol=1, iba=32, jba=32,
                   ipm=128, jpm=128, bpw=512, w0=4, w0h=4, w0l=4, qi=1, bq=8))
SCRATCH.update(_sb("float32", xf=32, bias=1, pm=128, low=4, qcol=1, one32=48, r11=48, mask=64, m11=64, tq=8, oq=8))

SEMAPHORES = (["e%d" % _i for _i in range(110)] + ["arr%d" % _i for _i in range(7)] +
              ["lar0", "lar1", "larr", "oarr", "sentm", "sentl"])

WALK = {9: [10, 9, 8, 7, 6], 8: [10, 9], 7: [10, 9, 8], 6: [10, 9, 8, 7, 6],
        4: [5], 3: [5, 4], 2: ["5.4", 3], 1: ["5.4", "3.2"], 0: ["5.4", "3.2", 1]}
FIN = {9: [0], 8: [1], 7: [2], 6: [4, 3], 4: [0], 3: [1], 2: [1], 1: [1], 0: [2]}
JOIN = {"5.4": (5, 4), "3.2": (3, 2)}
SLOT = {9: 0, 10: 1, 7: 2, 8: 3, 6: 4, 4: 0, 2: 1, "3.2": 2, "5.4": 3, 1: 4, 3: 5, 5: 6}
WIN2 = {9: [7, 8, 6], 6: [7, 8, 6], 2: ["5.4", 3], 1: ["5.4"], 0: ["5.4", 1]}
MAPS_TO = {10: [[9, 6], [8, 7]], 9: [[6], [8, 7]], 8: [[7], [9, 6]], 7: [[9], [6]], 6: [[9]],
           5: [[3, 4]], 4: [[0], [1, 2, 3]], 3: [[2]], 2: [[0], [1]], 1: [[0]]}
ENTRIES_TO = {5: ("l0", "lar0", [[0], [1, 2]]), 3: ("l1", "lar1", [[0], [1]])}
LIST_TO = {11: [[9], [6, 7, 8]], 9: [[0], [1, 2]], 6: [[3, 4]]}
OFFS_TO = {11: 10, 6: 5}
TAB_EARLY = {11: 3, 10: 2, 9: 5, 8: 2, 7: 2, 6: 5, 0: 8, 1: 6, 2: 4.5}
TAB_MID = {10: 6, 5: 4}
FILLER = {9: 768}


def rank_program(g, core, T, topo):
    me = T.rank_of(core)
    if me is None:
        return
    V, S, PE, Y = g.vector, g.scalar, g.tensor, g.sync
    events = []

    def ev():
        e = {"s": T.sem["e%d" % len(events)], "n": 0, "w": 0}
        events.append(e)
        return e

    def inc(op, e, n=1):
        op.then_inc(e["s"], n)
        e["n"] += n

    def wait(q, *es):
        for e in es:
            if e["n"]:
                q.wait_ge(e["s"], e["n"])
                e["w"] = e["n"]

    sent = {"sentm": 0, "sentl": 0}

    def send(dsts, out, in_, rsem, lsem):
        cores = [T.cores[d] for d in dsts]
        m = topo.mask(core, cores[0])
        for c in cores:
            m &= topo.mask(core, c)
        ids = []
        for c in cores:
            rid, pid = topo.addr(c, core)
            ids.append(DstId(rid=rid, pnc=pid))
        g.remote_dma_fused([RemoteDMATransfer(dst_ids=ids, dma_engine_mask=m, remote_sem=T.sem[rsem],
                                              srcs=[in_], dsts=[out] * len(ids))], local_sem=T.sem[lsem])
        sent[lsem] += bin(m).count("1")

    def arrived(src):
        return bin(topo.mask(T.cores[src], core)).count("1")

    walk = WALK.get(me, [])
    has_map = 1 <= me <= 10
    own = me in walk
    first = walk[:1] == [10]
    two = me in WIN2
    in2 = WIN2.get(me, [])
    joins = [m for m in walk if m in JOIN]
    last = len(walk) - 1
    wide = [(t % 2 == 1) if first else (t % 2 == 0) for t in range(len(walk))]
    fin = FIN.get(me, [])
    forms = sorted(set("a" if wide[t] else "b" for t in fin))

    e_tab = []
    tab_at = [0]

    def tab_load(units):
        a = tab_at[0]
        b = min(8192, a + int(1024 * units))
        if b > a:
            e_tab.append(ev())
            inc(Y.dma_start(T.tabs[:, a:b], T.tab[:, a:b]), e_tab[-1], 16)
        tab_at[0] = b

    e_bp, e_st, e_bpw, e_st16, e_bpl, e_fil = ev(), ev(), ev(), ev(), ev(), ev()
    if has_map:
        inc(Y.dma_start(T.bps[0:64, :], T.bp[:]), e_bp, 16)
        inc(S.dma_start(T.bps[64:128, :], T.bp[:]), e_bp, 16)
    if me in ENTRIES_TO:
        for k in range(8):
            q = (Y, S)[k % 2]
            inc(q.dma_start(T.bpl[16 * k:16 * k + 16, :], T.bp[:, 64 * k:64 * k + 64]), e_bpl, 16)
    if me == 11:
        for q, gs in ((Y, (0, 1, 2, 3)), (S, (4, 5, 6, 7))):
            for k in gs:
                inc(q.dma_start(T.w0[16 * k:16 * k + 16, :], T.st[:, 4 * k:4 * k + 4]), e_st, 16)
            for k in gs:
                inc(q.dma_start(T.bpw[16 * k:16 * k + 16, :], T.bp[:]), e_bpw, 16)
        inc(Y.dma_start(T.st16[:], T.st[:]), e_st16, 16)
    if me in FILLER:
        inc(S.dma_start(T.win2[:, 8192 - FILLER[me]:8192], T.tab[:, 0:FILLER[me]]), e_fil, 16)
    tab_load(TAB_EARLY.get(me, 4))

    e_one, e_z, e_win, e_win2, e_store, h0 = ev(), ev(), ev(), ev(), ev(), ev()
    e_bias, e_sp, e_pc, e_io = ev(), ev(), ev(), ev()
    if has_map:
        inc(V.memset(T.bias[0:64, :], 0.0), e_bias)
        inc(V.memset(T.bias[64:128, :], -256.0), e_bias)
    if walk:
        inc(V.memset((T.win2 if two else T.win)[:, 0:2048], 0.0), e_z)
    if two:
        wait(S, e_z)
        inc(S.activation(T.win[:, 6144:8192], T.win2[:, 0:2048], COPY), e_win)
        inc(S.activation(T.win2[:, 4608:6656], T.win2[:, 0:2048], COPY), e_win2)
        if not joins:
            n = 1536 - FILLER.get(me, 0)
            inc(S.activation(T.win2[:, 6656:6656 + n], T.win2[:, 0:n], COPY), e_win2)
    if has_map:
        wait(V, e_bp)
        inc(V.tensor_scalar(T.sp[0:64, :], T.bps[0:64, :], 15, None, AND), e_sp)
        inc(V.tensor_scalar(T.sp[64:128, :], T.bps[64:128, :], 4, None, SHR), e_sp)
        wait(V, e_sp, e_bias)
        inc(V.tensor_scalar(T.pc[:], T.sp[:], T.bias[:, 0:1], None, ADD), e_pc)
        wait(g, e_pc)
        r = SLOT[me]
        for dsts in MAPS_TO[me]:
            send(dsts, T.land[128 * r:128 * r + 128, :], T.pc[:], "arr%d" % r, "sentm")
        if own:
            wait(Y, e_pc)
            inc(Y.dma_start(T.mine[:], T.pc[:]), e_store, 16)
    if me in ENTRIES_TO:
        x1, x2, x3, x4 = ev(), ev(), ev(), ev()
        wait(V, e_bpl)
        inc(V.tensor_scalar(T.bl[:], T.bpl[:], 15, None, AND), x1)
        inc(V.tensor_scalar(T.bh[:], T.bpl[:], 4, None, SHR), x2)
        wait(V, x1)
        inc(V.tensor_scalar(T.bm[:], T.bl[:], 512.0, None, MUL), x2)
        wait(V, x2)
        inc(V.tensor_tensor(T.bo[:], T.bm[:], T.bh[:], ADD), x3)
        wait(V, x3)
        inc(V.tensor_copy(T.ol[:], T.bo[:]), x4)
        wait(g, x4)
        buf, sm, calls = ENTRIES_TO[me]
        for dsts in calls:
            send(dsts, T[buf][:], T.ol[:], sm, "sentm")
    if walk:
        inc(V.memset(T.one[:, 0:64], 1.0), e_one)
        inc(V.memset(T.one[:, 64:128], 16.0), e_one)
        if any(wide[:-1]):
            inc(V.memset(T.off_a[64:128, :], 0), h0)
    if two:
        inc(V.memset(T.win[:, 0:6144], 0.0), e_win)
        inc(V.memset(T.win2[:, 2048:4608], 0.0), e_win2)
        if joins:
            inc(V.memset(T.win2[:, 6656:8192], 0.0), e_win2)
    elif walk:
        inc(V.memset(T.win[:, 2048:8192], 0.0), e_win)

    e_rw, e_rwf, e_jp, e_pmb, e_bm = ev(), ev(), ev(), ev(), ev()

    def kind(t):
        if t < last:
            return "v" if walk[t + 1] in JOIN else "o"
        if me in LIST_TO:
            return "v" if WALK[LIST_TO[me][0][0]][0] in JOIN else "o"
        return None

    if walk:
        wait(g, e_one)
        todo = sorted((SLOT[walk[t]], kind(t)) for t in range(len(walk)) if kind(t))
        runs = []
        for s, k in todo:
            if runs and runs[-1][2] == k and runs[-1][0] + runs[-1][1] == s:
                runs[-1][1] += 1
            else:
                runs.append([s, 1, k])
        e_r0 = ev()
        for s, n, k in runs:
            out, one = T.rwm[:, 8 * s:8 * (s + n)], T.one[:, 0:8 * n]
            inc(g.affine_select(out, one, [[-2, n], [-16, 8]], EQ, 0.0, -2 * s - (1 if k == "o" else 0), 1), e_r0)
        wait(g, e_r0)
        for s, n, k in runs:
            out = T.rwm[:, 8 * s:8 * (s + n)]
            inc(g.affine_select(out, out, [[-2, n], [-16, 8]], NE, 512.0 if k == "o" else 16.0,
                                -2 * s - (0 if k == "o" else 1), 1), e_rw)
        inc(g.iota(T.ipm[:], [[1, 128]], 128, -1), e_io)
        for i, t in enumerate(fin):
            pat = [[-16, 8], [0, 4]] if wide[t] else [[0, 8], [-16, 4]]
            s = SLOT[walk[t]]
            inc(g.affine_select(T.rwf[:, 64 * i:64 * i + 32], T.one[:, 0:32], pat, EQ, 0.0, -2 * s, 1), e_rwf)
            inc(g.affine_select(T.rwf[:, 64 * i + 32:64 * i + 64], T.one[:, 64:96], pat, EQ, 0.0, -2 * s - 1, 1), e_rwf)
        e_b0 = ev()
        pats = {"a": ([[0, 16], [-16, 4]], [[0, 16], [16, 4]]), "b": ([[0, 2], [-16, 8], [0, 4]], [[0, 2], [16, 8], [0, 4]])}
        for f in forms:
            b = T["bm" + f]
            inc(g.affine_select(b[:], T.one[:, 0:64], pats[f][0], GE, 0.0, 0, 1), e_b0)
        wait(g, e_b0)
        for f in forms:
            b = T["bm" + f]
            inc(g.affine_select(b[:], b[:], pats[f][1], GE, 0.0, 15, -1), e_bm)
        wait(V, e_io)
        inc(V.tensor_scalar(T.jpm[:], T.ipm[:], 15, None, AND), e_jp)
        wait(V, e_jp)
        inc(V.tensor_scalar(T.pmb[:], T.jpm[:], 0.0, None, EQ), e_pmb)

    e_wdma, e_wdma2 = ev(), ev()
    if has_map and TAB_MID.get(me):
        Y.wait_ge(T.sem.sentm, sent["sentm"])
        tab_load(TAB_MID[me])

    def fill(q, gp, s0, s1, src, second):
        w, e = (T.win2, e_wdma2) if second else (T.win, e_wdma)
        inc(q.dma_start(w[16 * gp + 2 * s0:16 * gp + 2 * s1, :], src), e, 16)

    def groups_of(m):
        return range(8) if m not in walk or wide[walk.index(m)] else range(4)

    def fill_mine():
        wait(Y, e_store)
        for gp in groups_of(me):
            fill(Y, gp, SLOT[me], SLOT[me] + 1, T.mine[:], me in in2)

    def fill_got(got, qs):
        for m in got:
            for q in qs:
                q.wait_ge(T.sem["arr%d" % SLOT[m]], arrived(m))
        for gp in range(8):
            rs = sorted(SLOT[m] for m in got if gp in groups_of(m))
            i = 0
            while i < len(rs):
                k = i
                while k + 1 < len(rs) and rs[k + 1] == rs[k] + 1:
                    k += 1
                fill(qs[gp % len(qs)], gp, rs[i], rs[k] + 1, T.land[128 * rs[i]:128 * (rs[k] + 1), :], got[0] in in2)
                i = k + 1

    if walk:
        qs = (Y,) if me in LIST_TO else (Y, S)
        for q in qs:
            wait(q, e_win, e_z)
        if joins:
            fill_got(sorted((JOIN[m][1] for m in joins), reverse=True), qs)
        elif two:
            if own and me not in in2:
                fill_mine()
            fill_got([m for m in walk if m != me and m not in in2], qs)
        else:
            fill_got(walk, qs)
    if two:
        rest = [m for m in in2 if m != me and m not in JOIN]
        if rest:
            for q in (Y, S):
                wait(q, e_z, e_win, e_win2, e_fil)
            fill_got(rest, (Y,) if joins else (Y, S))
        if own and me in in2:
            fill_mine()

    e_cp, e_join = [], {}
    if joins:
        wait(V, e_wdma)
        wait(S, e_wdma)
        for i, m in enumerate(joins):
            x, y = JOIN[m]
            e = ev()
            e_cp.append(e)
            lst, out = T["l%d" % i], T["cmp%d" % i]
            for q in (V, S):
                q.wait_ge(T.sem["lar%d" % i], arrived(x))
            inc(V.tensor_copy(out[:, 0:512], T.win[:, :].indirect(lst[:, 0:32])), e)
            inc(S.activation(out[:, 512:1024], T.win[:, :].indirect(lst[:, 32:64]), COPY), e)
        for i, m in enumerate(joins):
            qs = (Y,) if i == 0 and len(joins) > 1 else (Y, S)
            second = m in in2
            for q in qs:
                wait(q, *e_cp[0:i + 1])
                if second:
                    wait(q, e_win, e_win2)
            e_join[m] = ev()
            a, n = 2 * SLOT[JOIN[m][1]], 0
            for gp in groups_of(m):
                for k in (0, 1):
                    o = 16 * gp + 2 * SLOT[m] + k
                    inc(qs[n % len(qs)].dma_start((T.win2 if second else T.win)[o:o + 1, :], T["cmp%d" % i][a + k:128:16, :]),
                        e_join[m], 16)
                    n += 1
    if me != 11:
        tab_load(8)

    offs = None
    e_offs = []
    if walk:
        up = 11 if first else (9 if me <= 2 else 6)
        off, c0 = (T.lsta if first else T.lstb), 0
        e_off = None
        wait(PE, e_rw)
        wait(V, h0)
        seen = []
        for t, m in enumerate(walk):
            x = 128 * t
            w, k = (8, 64) if wide[t] else (4, 128)
            h = k // 2
            win = T.win2 if m in in2 else T.win
            e_g, e_m = ev(), ev()
            ready = [e_wdma2, e_win2, e_fil] if m in in2 else [e_wdma, e_win, e_z]
            ready += [e_join[j] for j in joins if (j in in2) == (m in in2)]
            for q in (V, S):
                if (m in in2) not in seen:
                    wait(q, *ready)
                if e_off is None:
                    q.wait_ge(T.sem.larr, arrived(up))
                else:
                    wait(q, e_off)
            seen.append(m in in2)
            inc(V.tensor_copy(T.gat[:, x:x + h], win[:, :].indirect(off[:, c0:c0 + h // 16])), e_g)
            inc(S.activation(T.gat[:, x + h:x + k], win[:, :].indirect(off[:, c0 + h // 16:c0 + k // 16]), COPY), e_g)
            wait(PE, e_g)
            kd = kind(t)
            if kd:
                s = 8 * SLOT[m]
                inc(PE.matmul(T.ps[0:k, 512 * t:512 * t + w], T.gat[:, x:x + k], T.rwm[:, s:s + w], True, True), e_m)
                wait(V, e_m)
                off, c0 = (T.off_a, 8 * t) if wide[t] else (T.off_b, 4 * t)
                e_off = ev()
                inc(V.tensor_scalar(off[0:k, c0:c0 + w], T.ps[0:k, 512 * t:512 * t + w], 256.0 if kd == "o" else 4096.0, None, ADD),
                    e_off)
        if me in LIST_TO:
            wait(g, e_off)
            for dsts in LIST_TO[me]:
                send(dsts, T.lstb[:], off[:, c0:c0 + 4], "larr", "sentl")
        wait(PE, e_rwf, e_pmb)
        if e_off is not None:
            wait(PE, e_off)
        wait(V, e_bm)
        for i, t in enumerate(fin):
            k, f = (64, "a") if wide[t] else (128, "b")
            x, pf = T.xb[0:k, 64 * i:64 * i + 64], T.pf[:, 512 * i:512 * i + 32]
            pt = T.ps[0:k, 512 * t + 64:512 * t + 128]
            e0, e1, e2, e3 = ev(), ev(), ev(), ev()
            inc(PE.matmul(pt, T.gat[:, 128 * t:128 * t + k], T.rwf[:, 64 * i:64 * i + 64], True, True), e0)
            wait(V, e0)
            inc(V.tensor_tensor(x, pt, T["bm" + f][0:k, :], MUL), e1)
            wait(PE, e1)
            PE.matmul(pf, T.pmb[0:k, :], T.xb[0:k, 64 * i:64 * i + 32], True, False)
            inc(PE.matmul(pf, T.pmb[0:k, :], T.xb[0:k, 64 * i + 32:64 * i + 64], False, True), e2)
            wait(V, e2)
            inc(V.tensor_scalar(T.of[:, 32 * i:32 * i + 32], pf, 4096.0, None, ADD), e3)
            if me == 6 and i == 0:
                wait(g, e3)
                send([OFFS_TO[me]], T.ofl[:], T.of[:, 0:32], "oarr", "sentl")
            else:
                offs, e_offs = (T.of, 32 * i), [e3]

    if me == 11:
        a1, a3, a4, a5, b0, b1, b2, b3 = ev(), ev(), ev(), ev(), ev(), ev(), ev(), ev()
        inc(V.memset(T.off_a[64:128, 0:8], 0), h0)
        inc(V.memset(T.one[:], 1.0), b0)
        inc(V.memset(T.one32[:], 1.0), b1)
        wait(V, b1)
        inc(V.memset(T.one32[:, 8:16], 512.0), b2)
        inc(g.iota(T.kcol[:], [[0, 1]], 0, 1), a1)
        inc(g.iota(T.ipm[:], [[1, 128]], 128, -1), a1)
        c1, c2, c3, c4 = ev(), ev(), ev(), ev()
        wait(g, b0)
        inc(g.affine_select(T.blk[:], T.one[:], [[-16, 8], [0, 16]], GE, 0.0, 0, 1), c1)
        wait(g, c1)
        inc(g.affine_select(T.blk[:], T.blk[:], [[16, 8], [0, 16]], GE, 0.0, 15, -1), c2)
        wait(g, b1, b2)
        inc(g.affine_select(T.r11[:, 0:16], T.one32[:, 0:16], [[0, 2], [-16, 8]], GE, 0.0, 0, 1), c3)
        inc(g.affine_select(T.r11[:, 16:48], T.one32[:, 16:48], [[-16, 8], [0, 4]], GE, 0.0, 0, 1), c3)
        wait(g, c3)
        inc(g.affine_select(T.r11[:, 0:16], T.r11[:, 0:16], [[0, 2], [16, 8]], GE, 0.0, 15, -1), c4)
        inc(g.affine_select(T.r11[:, 16:48], T.r11[:, 16:48], [[16, 8], [0, 4]], GE, 0.0, 15, -1), c4)
        inc(g.iota(T.iba[:, 0:32], [[0, 8], [16, 4]], 15, -1), a5)
        wait(V, a1)
        inc(V.tensor_scalar(T.qi[:], T.kcol[:], 15, None, AND), a3)
        inc(V.tensor_scalar(T.jpm[:], T.ipm[:], 15, None, AND), a3)
        wait(V, a3)
        inc(V.tensor_copy(T.qcol[:], T.qi[:]), a4)
        inc(V.tensor_scalar(T.e16[:], T.jpm[:, 0:16], 0.0, None, EQ), a4)
        e1, e2, e3, e4, e5, e6, e7 = ev(), ev(), ev(), ev(), ev(), ev(), ev()
        wait(V, e_st)
        inc(V.tensor_scalar(T.w0l[:], T.w0[:], 15, None, AND), e1)
        inc(V.tensor_scalar(T.w0h[:], T.w0[:], 4, None, SHR), e2)
        wait(V, e1)
        inc(V.tensor_copy(T.low[:], T.w0l[:]), e3)
        for q, cs in ((V, (0, 1)), (S, (2, 3))):
            wait(q, a4, e3)
            for c in cs:
                if q is V:
                    inc(V.tensor_scalar(T.xl[:, 16 * c:16 * c + 16], T.e16[:], T.low[:, c:c + 1], None, MUL), e5)
                else:
                    inc(S.activation(T.xl[:, 16 * c:16 * c + 16], T.e16[:], COPY, scale=T.low[:, c:c + 1]), e5)
        wait(V, e2)
        inc(V.tensor_copy(T.off0[:], T.w0h[:]), e4)
        wait(PE, c2, e5)
        inc(PE.matmul(T.ps[:, 512:576], T.blk[:], T.xl[:], True, True), e6)
        wait(V, e6)
        inc(V.tensor_scalar(T.mask[:], T.ps[:, 512:576], T.qcol[:, 0:1], None, EQ), e7)
        h1, h2, h3, h4, h5, h6 = ev(), ev(), ev(), ev(), ev(), ev()
        wait(V, e7, e4, e_bpw)
        inc(V.tensor_tensor(T.m11[:], T.bpw[:, :].indirect(T.off0[:, 0:4]), T.mask[:], MUL), h1)
        wait(PE, c4, h1)
        inc(PE.matmul(T.ps[0:64, 0:48], T.m11[:], T.r11[:], True, True), h2)
        wait(V, h2)
        inc(V.tensor_scalar(T.bq[0:64, :], T.ps[0:64, 0:8], 0.0625, -0.46875, MUL, ADD), h3)
        wait(V, h3)
        inc(V.tensor_scalar(T.tq[0:64, :], T.bq[0:64, :], -8191.0, None, MUL), h4)
        wait(V, h4)
        inc(V.tensor_tensor(T.oq[0:64, :], T.tq[0:64, :], T.ps[0:64, 8:16], ADD), h5)
        wait(V, h5)
        inc(V.tensor_copy(T.off_a[0:64, 0:8], T.oq[0:64, :]), h6)
        wait(g, h0, h6)
        for dsts in LIST_TO[me]:
            send(dsts, T.lsta[:], T.off_a[:, 0:8], "larr", "sentl")
        k0, k1, k2, k3, k4, k5, k6 = ev(), ev(), ev(), ev(), ev(), ev(), ev()
        wait(V, a5)
        inc(V.tensor_scalar(T.jba[:, 0:32], T.iba[:, 0:32], 4, None, SHR), k0)
        inc(V.tensor_scalar(T.pm[:], T.jpm[:], 0.0, None, EQ), b3)
        wait(V, k0)
        inc(V.tensor_scalar(T.bma[:, 0:32], T.jba[:, 0:32], 0.0, None, EQ), k1)
        wait(V, k1)
        inc(V.tensor_tensor(T.xf[0:64, :], T.ps[0:64, 16:48], T.bma[0:64, 0:32], MUL), k2)
        wait(PE, b3, k2)
        inc(PE.matmul(T.pf[:, 0:32], T.pm[0:64, :], T.xf[0:64, :], True, True), k3)
        wait(V, k3)
        inc(V.tensor_copy(T.of[:, 0:32], T.pf[:, 0:32]), k4)
        wait(g, k4)
        send([OFFS_TO[me]], T.ofl[:], T.of[:, 0:32], "oarr", "sentl")
        wait(V, e_st16)
        inc(V.tensor_copy(T.stf[:], T.st16[:]), k5)
        wait(PE, k5)
        inc(PE.matmul(T.pf[:, 512:544], T.pm[0:16, :], T.stf[:], True, True), k6)
        e_offs = [ev()]
        wait(V, k6)
        inc(V.tensor_copy(T.of[:, 32:64], T.pf[:, 512:544]), e_offs[0])
        offs = (T.of, 32)
        Y.wait_ge(T.sem.sentl, sent["sentl"])
        tab_load(8)

    e_y0, e_y1, e_out = ev(), ev(), ev()
    for q in (V, S):
        if offs is None:
            q.wait_ge(T.sem.oarr, arrived(11 if me == 10 else 6))
        wait(q, *(e_offs + e_tab))
    o, c0 = (T.ofl, 0) if offs is None else offs
    inc(V.tensor_copy(T.ysb[:, 0:256], T.tabs[:, :].indirect(o[:, c0:c0 + 16])), e_y0)
    inc(S.activation(T.ysb[:, 256:512], T.tabs[:, :].indirect(o[:, c0 + 16:c0 + 32]),
                     ActivationFunctionType.Identity, bias=-0.0), e_y1)
    wait(Y, e_y0)
    inc(Y.dma_start(T.y[:, 0:256], T.ysb[:, 0:256]), e_out, 16)
    wait(S, e_y1)
    inc(S.dma_start(T.y[:, 256:512], T.ysb[:, 256:512]), e_out, 16)
    wait(g, e_out)
    for k in ("sentm", "sentl"):
        if sent[k]:
            g.wait_ge(T.sem[k], sent[k])
    for e in events:
        if e["w"] < e["n"]:
            wait(g, e)
